import numpy as np
import ml_dtypes


def mxq(x, axis, fmt="e4m3"):
    dtype, down = {"e4m3": (ml_dtypes.float8_e4m3fn, 7), "e5m2": (ml_dtypes.float8_e5m2, 14)}[fmt]
    v = np.moveaxis(np.asarray(x, np.float32).astype(ml_dtypes.bfloat16).astype(np.float64), axis, -1)
    blocks = v.reshape(v.shape[:-1] + (-1, 32))
    amax = np.abs(blocks).max(-1, keepdims=True)
    byte = np.maximum(np.where(amax > 0, np.frexp(amax)[1] - 1 + 127, 0) - down, 1)
    scale = np.exp2(byte - 127.0)
    codes = (blocks / scale).astype(np.float32).astype(dtype).astype(np.float64)
    return np.moveaxis((codes * scale).reshape(v.shape), -1, axis)


WIDE = False


def mx_kscale(k):
    if not WIDE:
        return np.ones(k)
    levels = np.array([10, -10, 5, -5, 0])
    if k % 512:
        return np.exp2(np.random.permutation(np.resize(levels, k // 32))).repeat(32)
    a = np.empty((k // 512, 16))
    for p in range(k // 512):
        a[p, :8] = np.random.permutation(np.resize(levels, 8))
        for g in range(8):
            far = levels[np.abs(levels - a[p, g]) >= 10]
            a[p, g + 8] = far[np.random.randint(len(far))]
    return np.exp2(a.ravel()).repeat(32)


def f64(x):
    return np.asarray(x).astype(np.float64)


def striped(idx):
    return np.tile(idx.reshape(-1, 16).T, (8, 1)).astype(np.uint16)


def unstriped(offs):
    return offs[:16].T.reshape(-1).astype(np.int64)


def pack_weight(w):
    k, n = w.shape
    w = f64(np.asarray(w, np.float32).astype(ml_dtypes.bfloat16)).reshape(k // 32, 32, n)
    amax = np.abs(w).max(1)
    byte = np.clip(np.where(amax > 0, np.frexp(amax)[1] - 1 + 127 - 7, 1), 1, 254)
    scaled = (w * np.exp2(127.0 - byte)[:, None, :]).reshape(k, n).astype(np.float32)
    words = np.ascontiguousarray(scaled.reshape(k // 512, 128, 4, n).transpose(0, 1, 3, 2)).astype(ml_dtypes.float8_e4m3fn).view(np.uint8)
    return words, np.ascontiguousarray(byte.astype(np.uint8).reshape(k // 512, 16, n))


def unpack_weight(words, scales):
    g, p, n, _ = words.shape
    vals = np.ascontiguousarray(words).view(ml_dtypes.float8_e4m3fn).astype(np.float64) * np.repeat(np.exp2(scales.astype(np.float64) - 127.0), 8, axis=1)[..., None]
    return vals.transpose(0, 1, 3, 2).reshape(g * 512, n)


K, T, S, D, V, N = 512, 4096, 1024, 3, 512, 256
P = 2 ** 7


def setup_inputs():
    n = np.random.standard_normal
    s = mx_kscale(K)[:, None]
    packed_xT = pack_weight(n((K, T)) * s)
    return {
        "x_words": packed_xT[0],
        "x_scales": packed_xT[1],
        "w1": (n((K, N)) / np.sqrt(K) / s).astype(np.float32),
        "gate": (np.tile(np.random.uniform(0.2, 1.0, (D, 1, V)) / np.sqrt(D), (1, P, 1))).astype(np.float32),
        "offs": striped(np.random.permutation(T)[:S]),
        "cen": striped(np.random.permutation(S)[:V]),
        "pos1": striped(np.random.permutation(S)[:V]),
        "pos2": striped(np.random.permutation(S)[:V]),
        "pos3": striped(np.random.permutation(S)[:V]),
    }


def reference(x_words, x_scales, w1, gate, offs, cen, pos1, pos2, pos3):
    xq = unpack_weight(x_words, x_scales)[:, unstriped(offs)]
    y = mxq(f64(w1), 0, "e4m3").T @ xq
    yc = y[:, unstriped(cen)]
    return yc + (y[:, unstriped(pos1)] - yc) * f64(gate)[0, :1] + (y[:, unstriped(pos2)] - yc) * f64(gate)[1, :1] + (y[:, unstriped(pos3)] - yc) * f64(gate)[2, :1]

@@ -1,0 +1,142 @@
+from contextlib import ExitStack
+
+import concourse.mybir as mybir
+from concourse.masks import make_identity
+
+K, T, S, D, V, N = 512, 4096, 1024, 3, 512, 256
+P = 128
+PACK = 4
+HALF = S // 2
+FLOPS = 2 * K * N * S
+
+F32 = mybir.dt.float32
+BF16 = mybir.dt.bfloat16
+I32 = mybir.dt.int32
+U32 = mybir.dt.uint32
+U16 = mybir.dt.uint16
+U8 = mybir.dt.uint8
+FP8X4 = mybir.dt.float8_e4m3fn_x4
+ALU = mybir.AluOpType
+
+
+def tile_picked_grand_none_p_kernel(tc, x_words, x_scales, w1, gate, offs, cen, pos1, pos2, pos3, out):
+    nc = tc.nc
+    with ExitStack() as ctx:
+        keep = ctx.enter_context(tc.tile_pool(name="keep", bufs=1))
+        psum = ctx.enter_context(tc.psum_pool(name="psum", bufs=1))
+
+        def bank(b, name):
+            return psum.tile([P, 512], F32, name=name, tag=f"bank{b}")
+
+        offs_sb = keep.tile([P, S // 16], U16, name="offs_sb")
+        lists = [keep.tile([P, V // 16], U16, name=f"list{d}") for d in range(D + 1)]
+        words = keep.tile([P, T], U32, name="words", align_bytes=64)
+        scales = keep.tile([P, T], U8, name="scales", align_bytes=64)
+        w_raw = [keep.tile([P, PACK, P], F32, name=f"w_raw{m}") for m in range(2)]
+        coef_t = keep.tile([P, D + 1, 8], F32, name="coef_t")
+        ident = keep.tile([P, P], F32, name="ident")
+        w_rows = w1.rearrange("(p j) n -> p j n", j=PACK)
+
+        nc.vector.memset(scales[:].bitcast(I32), 0)
+        nc.sync.dma_start(offs_sb[:], offs)
+        nc.sync.dma_start(w_raw[0][:], w_rows[:, :, 0:P])
+        nc.sync.dma_start(words[:].bitcast(I32), x_words[0].rearrange("p n t -> p (n t)").bitcast(I32))
+        nc.scalar.dma_start(coef_t[:, 1:, 0:PACK], gate[:, 0, :].rearrange("d (p i) -> p d i", i=PACK))
+        for q in range(4):
+            nc.scalar.dma_start(scales[32 * q : 32 * q + 4, :].bitcast(I32), x_scales[0, 4 * q : 4 * q + 4, :].bitcast(I32))
+        nc.sync.dma_start(w_raw[1][:], w_rows[:, :, P : 2 * P])
+        for tile, src in zip(lists, (cen, pos1, pos2, pos3)):
+            nc.sync.dma_start(tile[:], src)
+
+        make_identity(nc, ident[:])
+        gsum = keep.tile([P, 2, PACK], F32, name="gsum")
+        nc.gpsimd.tensor_tensor(gsum[:, 0, :], coef_t[:, 1, 0:PACK], coef_t[:, 2, 0:PACK], ALU.add)
+        nc.gpsimd.tensor_tensor(gsum[:, 1, :], gsum[:, 0, :], coef_t[:, 3, 0:PACK], ALU.add)
+        nc.gpsimd.tensor_scalar(coef_t[:, 0, 0:PACK], gsum[:, 1, :], -1.0, 1.0, ALU.mult, ALU.add)
+
+        w_codes = [keep.tile([P, P], U32, name=f"w_codes{m}", align_bytes=64) for m in range(2)]
+        w_scales = [keep.tile([P, P], U8, name=f"w_scales{m}", align_bytes=64) for m in range(2)]
+        w_bf = [keep.tile([P, P, PACK], BF16, name=f"w_bf{m}", align_bytes=64) for m in range(2)]
+
+        def round_w(m):
+            nc.scalar.copy(w_bf[m][:], w_raw[m][:].rearrange("p j n -> p n j"))
+
+        def quantize_w(m):
+            nc.vector.quantize_mx(out=w_codes[m][:].bitcast(FP8X4), scales=w_scales[m][:], in_=w_bf[m][:].rearrange("p n j -> p (n j)"))
+
+        picked_scales = keep.tile([P, S], U8, name="picked_scales", align_bytes=64)
+        nc.vector.tensor_copy(picked_scales[:], scales[:].indirect(offs_sb[:]))
+        round_w(0)
+        quantize_w(0)
+
+        coef = [keep.tile([P, V], F32, name=f"coef{d}") for d in range(D + 1)]
+        for d in (1, 2, 3, 0):
+            spread = bank(d, f"spread{d}")
+            for i in range(PACK):
+                nc.tensor.transpose(spread[:, i * P : (i + 1) * P], coef_t[:, d, i : i + 1].to_broadcast([P, P]), ident[:])
+            nc.scalar.copy(coef[d][:].rearrange("q (p i) -> q p i", i=PACK), spread[:].rearrange("q (i p) -> q p i", i=PACK))
+
+        picked = [keep.tile([P, HALF], U32, name=f"picked{h}", align_bytes=64) for h in range(2)]
+        y = [keep.tile([P, S], F32, name=f"y{m}") for m in range(2)]
+
+        def project(m, b, lo, hi, engine_copy):
+            h = lo // HALF
+            acc = bank(b, f"acc{m}_{lo}")
+            nc.tensor.matmul_mx(
+                out=acc[:, 0 : hi - lo],
+                lhsT=w_codes[m][:].bitcast(FP8X4),
+                lhsT_scale=w_scales[m][:],
+                rhs=picked[h][:, lo - h * HALF : hi - h * HALF].bitcast(FP8X4),
+                rhs_scale=picked_scales[:, lo:hi],
+                start=True,
+                stop=True,
+            )
+            engine_copy(y[m][:, lo:hi], acc[:, 0 : hi - lo])
+
+        for h in range(2):
+            nc.vector.tensor_copy(picked[h][:], words[:].indirect(offs_sb[:, h * HALF // 16 : (h + 1) * HALF // 16]))
+        round_w(1)
+        project(0, 4, 0, 512, nc.scalar.copy)
+        quantize_w(1)
+        project(0, 5, 512, 768, nc.vector.tensor_copy)
+        project(0, 6, 768, 1024, nc.scalar.copy)
+        project(1, 7, 0, 512, nc.scalar.copy)
+        project(1, 0, 512, 1024, nc.scalar.copy)
+
+        terms = [[keep.tile([P, V], F32, name=f"term{m}_{d}") for d in range(D + 1)] for m in range(2)]
+        sum_banks = ((1, 2, 3, 4), (5, 6, 7, 0))
+        sums = [[None] * 4, [None] * 4]
+        last = (3, 2)
+
+        def fetch(m, d):
+            nc.vector.tensor_tensor(terms[m][d][:], y[m][:].indirect(lists[d][:]), coef[d][:], ALU.mult)
+
+        def add_up(m, d):
+            for b in range(4):
+                if d == 0:
+                    sums[m][b] = bank(sum_banks[m][b], f"sum{m}_{b}")
+                nc.tensor.matmul(sums[m][b][:, 0:P], terms[m][d][:, b * P : (b + 1) * P], ident[:], start=(d == 0), stop=(d == last[m]), is_transpose=True)
+
+        def turn_back(m):
+            turned = keep.tile([P, V], F32, name=f"turned{m}")
+            for b in range(4):
+                nc.scalar.copy(turned[:, b * P : (b + 1) * P], sums[m][b][:, 0:P])
+            back = bank(sum_banks[m][0], f"back{m}")
+            for b in range(4):
+                nc.tensor.transpose(back[:, b * P : (b + 1) * P], turned[:, b * P : (b + 1) * P], ident[:])
+            return back
+
+        res = [keep.tile([P, V], F32, name=f"res{m}") for m in range(2)]
+        for m, d in ((0, 0), (0, 1), (1, 0), (1, 1), (1, 2)):
+            fetch(m, d)
+            add_up(m, d)
+        back1 = turn_back(1)
+        for m, d in ((0, 2), (0, 3)):
+            fetch(m, d)
+            add_up(m, d)
+        back0 = turn_back(0)
+        fetch(1, 3)
+        nc.scalar.copy(res[0][:], back0[:])
+        nc.scalar.dma_start(out[0:P, :], res[0][:])
+        nc.vector.tensor_tensor(res[1][:], back1[:], terms[1][3][:], ALU.add)
+        nc.sync.dma_start(out[P : 2 * P, :], res[1][:])

@@ -32,21 +32,22 @@ def tile_picked_grand_none_p_kernel(tc, x_words, x_scales, w1, gate, offs, cen, 
         lists = [keep.tile([P, V // 16], U16, name=f"list{d}") for d in range(D + 1)]
         words = keep.tile([P, T], U32, name="words", align_bytes=64)
         scales = keep.tile([P, T], U8, name="scales", align_bytes=64)
-        w_raw = [keep.tile([P, PACK, P], F32, name=f"w_raw{m}") for m in range(2)]
+        planes = keep.tile([P, S], U8, name="planes", align_bytes=64)
+        w_raw = keep.tile([P, PACK, N], F32, name="w_raw")
         coef_t = keep.tile([P, D + 1, 8], F32, name="coef_t")
         ident = keep.tile([P, P], F32, name="ident")
-        w_rows = w1.rearrange("(p j) n -> p j n", j=PACK)
 
         nc.vector.memset(scales[:].bitcast(I32), 0)
+        nc.vector.memset(planes[:].bitcast(I32), 0)
         nc.sync.dma_start(offs_sb[:], offs)
-        nc.sync.dma_start(w_raw[0][:], w_rows[:, :, 0:P])
-        nc.sync.dma_start(words[:].bitcast(I32), x_words[0].rearrange("p n t -> p (n t)").bitcast(I32))
         nc.scalar.dma_start(coef_t[:, 1:, 0:PACK], gate[:, 0, :].rearrange("d (p i) -> p d i", i=PACK))
-        for q in range(4):
-            nc.scalar.dma_start(scales[32 * q : 32 * q + 4, :].bitcast(I32), x_scales[0, 4 * q : 4 * q + 4, :].bitcast(I32))
-        nc.sync.dma_start(w_raw[1][:], w_rows[:, :, P : 2 * P])
-        for tile, src in zip(lists, (cen, pos1, pos2, pos3)):
-            nc.sync.dma_start(tile[:], src)
+        nc.sync.dma_start(w_raw[:], w1.rearrange("(p j) n -> p j n", j=PACK))
+        nc.sync.dma_start(lists[0][:], cen)
+        nc.sync.dma_start(lists[1][:], pos1)
+        nc.scalar.dma_start(scales[0:P:8, :].bitcast(I32), x_scales[0].bitcast(I32))
+        nc.sync.dma_start(words[:].bitcast(I32), x_words[0].rearrange("p n t -> p (n t)").bitcast(I32))
+        nc.sync.dma_start(lists[2][:], pos2)
+        nc.sync.dma_start(lists[3][:], pos3)
 
         make_identity(nc, ident[:])
         gsum = keep.tile([P, 2, PACK], F32, name="gsum")
@@ -59,15 +60,18 @@ def tile_picked_grand_none_p_kernel(tc, x_words, x_scales, w1, gate, offs, cen, 
         w_bf = [keep.tile([P, P, PACK], BF16, name=f"w_bf{m}", align_bytes=64) for m in range(2)]
 
         def round_w(m):
-            nc.scalar.copy(w_bf[m][:], w_raw[m][:].rearrange("p j n -> p n j"))
+            nc.scalar.copy(w_bf[m][:], w_raw[:, :, m * P : (m + 1) * P].rearrange("p j n -> p n j"))
 
         def quantize_w(m):
             nc.vector.quantize_mx(out=w_codes[m][:].bitcast(FP8X4), scales=w_scales[m][:], in_=w_bf[m][:].rearrange("p n j -> p (n j)"))
 
         picked_scales = keep.tile([P, S], U8, name="picked_scales", align_bytes=64)
         nc.vector.tensor_copy(picked_scales[:], scales[:].indirect(offs_sb[:]))
-        round_w(0)
-        quantize_w(0)
+        for i in range(4):
+            nc.sync.dma_start(planes[i:P:32, :].bitcast(I32), picked_scales[8 * i : P : 32, :].bitcast(I32))
+        for m in range(2):
+            round_w(m)
+            quantize_w(m)
 
         coef = [keep.tile([P, V], F32, name=f"coef{d}") for d in range(D + 1)]
         for d in (1, 2, 3, 0):
@@ -87,7 +91,7 @@ def tile_picked_grand_none_p_kernel(tc, x_words, x_scales, w1, gate, offs, cen, 
                 lhsT=w_codes[m][:].bitcast(FP8X4),
                 lhsT_scale=w_scales[m][:],
                 rhs=picked[h][:, lo - h * HALF : hi - h * HALF].bitcast(FP8X4),
-                rhs_scale=picked_scales[:, lo:hi],
+                rhs_scale=planes[:, lo:hi],
                 start=True,
                 stop=True,
             )
@@ -95,48 +99,61 @@ def tile_picked_grand_none_p_kernel(tc, x_words, x_scales, w1, gate, offs, cen, 
 
         for h in range(2):
             nc.vector.tensor_copy(picked[h][:], words[:].indirect(offs_sb[:, h * HALF // 16 : (h + 1) * HALF // 16]))
-        round_w(1)
         project(0, 4, 0, 512, nc.scalar.copy)
-        quantize_w(1)
         project(0, 5, 512, 768, nc.vector.tensor_copy)
         project(0, 6, 768, 1024, nc.scalar.copy)
         project(1, 7, 0, 512, nc.scalar.copy)
         project(1, 0, 512, 1024, nc.scalar.copy)
 
-        terms = [[keep.tile([P, V], F32, name=f"term{m}_{d}") for d in range(D + 1)] for m in range(2)]
+        terms = [[keep.tile([P, V], F32, name=f"term{m}_{d}") for d in range(D)] for m in range(2)]
+        terms[0].append(terms[1][1])
+        terms[1].append(terms[1][2])
         sum_banks = ((1, 2, 3, 4), (5, 6, 7, 0))
         sums = [[None] * 4, [None] * 4]
-        last = (3, 2)
+        turned = [keep.tile([P, V], F32, name=f"turned{m}") for m in range(2)]
+        res = [keep.tile([P, V], F32, name=f"res{m}") for m in range(2)]
+        H = V // 2
 
-        def fetch(m, d):
-            nc.vector.tensor_tensor(terms[m][d][:], y[m][:].indirect(lists[d][:]), coef[d][:], ALU.mult)
+        def fetch(m, d, lo, hi):
+            nc.vector.tensor_tensor(terms[m][d][:, lo:hi], y[m][:].indirect(lists[d][:, lo // 16 : hi // 16]), coef[d][:, lo:hi], ALU.mult)
 
-        def add_up(m, d):
-            for b in range(4):
+        def add_up(m, d, blocks):
+            for b in blocks:
                 if d == 0:
                     sums[m][b] = bank(sum_banks[m][b], f"sum{m}_{b}")
-                nc.tensor.matmul(sums[m][b][:, 0:P], terms[m][d][:, b * P : (b + 1) * P], ident[:], start=(d == 0), stop=(d == last[m]), is_transpose=True)
+                last = D if (m == 0 and b < 2) else D - 1
+                nc.tensor.matmul(sums[m][b][:, 0:P], terms[m][d][:, b * P : (b + 1) * P], ident[:], start=(d == 0), stop=(d == last), is_transpose=True)
 
-        def turn_back(m):
-            turned = keep.tile([P, V], F32, name=f"turned{m}")
-            for b in range(4):
-                nc.scalar.copy(turned[:, b * P : (b + 1) * P], sums[m][b][:, 0:P])
-            back = bank(sum_banks[m][0], f"back{m}")
-            for b in range(4):
-                nc.tensor.transpose(back[:, b * P : (b + 1) * P], turned[:, b * P : (b + 1) * P], ident[:])
+        def turn_back(m, h):
+            for b in (2 * h, 2 * h + 1):
+                nc.scalar.copy(turned[m][:, b * P : (b + 1) * P], sums[m][b][:, 0:P])
+            back = bank(sum_banks[m][2 * h], f"back{m}_{h}")
+            for b in range(2):
+                nc.tensor.transpose(back[:, b * P : (b + 1) * P], turned[m][:, (2 * h + b) * P : (2 * h + b + 1) * P], ident[:])
             return back
 
-        res = [keep.tile([P, V], F32, name=f"res{m}") for m in range(2)]
-        for m, d in ((0, 0), (0, 1), (1, 0), (1, 1), (1, 2)):
-            fetch(m, d)
-            add_up(m, d)
-        back1 = turn_back(1)
-        for m, d in ((0, 2), (0, 3)):
-            fetch(m, d)
-            add_up(m, d)
-        back0 = turn_back(0)
-        fetch(1, 3)
-        nc.scalar.copy(res[0][:], back0[:])
-        nc.scalar.dma_start(out[0:P, :], res[0][:])
-        nc.vector.tensor_tensor(res[1][:], back1[:], terms[1][3][:], ALU.add)
-        nc.sync.dma_start(out[P : 2 * P, :], res[1][:])
+        def finish(m, h):
+            cols = slice(h * H, (h + 1) * H)
+            nc.vector.tensor_tensor(res[m][:, cols], backs[m, h][:, 0:H], terms[m][D][:, cols], ALU.add)
+            nc.sync.dma_start(out[m * P : (m + 1) * P, cols], res[m][:, cols])
+
+        backs = {}
+        for m in range(2):
+            for d in range(D):
+                fetch(m, d, 0, V)
+                add_up(m, d, range(4))
+            if m == 0:
+                backs[0, 1] = turn_back(0, 1)
+        backs[1, 0] = turn_back(1, 0)
+        backs[1, 1] = turn_back(1, 1)
+        fetch(0, D, 0, H)
+        add_up(0, D, range(2))
+        backs[0, 0] = turn_back(0, 0)
+        nc.scalar.copy(res[0][:, 0:H], backs[0, 0][:, 0:H])
+        nc.scalar.dma_start(out[0:P, 0:H], res[0][:, 0:H])
+        fetch(0, D, H, V)
+        fetch(1, D, 0, H)
+        finish(0, 1)
+        fetch(1, D, H, V)
+        finish(1, 0)
+        finish(1, 1)

@@ -37,15 +37,15 @@ def tile_picked_grand_none_p_kernel(tc, x_words, x_scales, w1, gate, offs, cen, 
         coef_t = keep.tile([P, D + 1, 8], F32, name="coef_t")
         ident = keep.tile([P, P], F32, name="ident")
 
-        nc.vector.memset(scales[:].bitcast(I32), 0)
+        nc.vector.memset(scales[0:112, :].bitcast(I32), 0)
         nc.vector.memset(planes[:].bitcast(I32), 0)
         nc.sync.dma_start(offs_sb[:], offs)
+        nc.sync.dma_start(scales[112:P, :].bitcast(I32), x_scales[0].bitcast(I32))
         nc.scalar.dma_start(coef_t[:, 1:, 0:PACK], gate[:, 0, :].rearrange("d (p i) -> p d i", i=PACK))
         nc.sync.dma_start(w_raw[:], w1.rearrange("(p j) n -> p j n", j=PACK))
         nc.sync.dma_start(lists[0][:], cen)
-        nc.sync.dma_start(lists[1][:], pos1)
-        nc.scalar.dma_start(scales[0:P:8, :].bitcast(I32), x_scales[0].bitcast(I32))
         nc.sync.dma_start(words[:].bitcast(I32), x_words[0].rearrange("p n t -> p (n t)").bitcast(I32))
+        nc.sync.dma_start(lists[1][:], pos1)
         nc.sync.dma_start(lists[2][:], pos2)
         nc.sync.dma_start(lists[3][:], pos3)
 
@@ -68,7 +68,7 @@ def tile_picked_grand_none_p_kernel(tc, x_words, x_scales, w1, gate, offs, cen, 
         picked_scales = keep.tile([P, S], U8, name="picked_scales", align_bytes=64)
         nc.vector.tensor_copy(picked_scales[:], scales[:].indirect(offs_sb[:]))
         for i in range(4):
-            nc.sync.dma_start(planes[i:P:32, :].bitcast(I32), picked_scales[8 * i : P : 32, :].bitcast(I32))
+            nc.sync.dma_start(planes[i:P:32, :].bitcast(I32), picked_scales[112 + i : P : 4, :].bitcast(I32))
         for m in range(2):
             round_w(m)
             quantize_w(m)

@@ -34,26 +34,32 @@ def tile_picked_grand_none_p_kernel(tc, x_words, x_scales, w1, gate, offs, cen, 
         scales = keep.tile([P, T], U8, name="scales", align_bytes=64)
         planes = keep.tile([P, S], U8, name="planes", align_bytes=64)
         w_raw = keep.tile([P, PACK, N], F32, name="w_raw")
-        coef_t = keep.tile([P, D + 1, 8], F32, name="coef_t")
+        gate_rows = keep.tile([P, D, P], F32, name="gate_rows")
+        coef_t = keep.tile([P, D + 1, 4], F32, name="coef_t")
         ident = keep.tile([P, P], F32, name="ident")
 
         nc.vector.memset(scales[0:112, :].bitcast(I32), 0)
+        nc.vector.memset(gate_rows[0 : P - 4, :, :], 0.0)
         nc.vector.memset(planes[:].bitcast(I32), 0)
         nc.sync.dma_start(offs_sb[:], offs)
         nc.sync.dma_start(scales[112:P, :].bitcast(I32), x_scales[0].bitcast(I32))
-        nc.scalar.dma_start(coef_t[:, 1:, 0:PACK], gate[:, 0, :].rearrange("d (p i) -> p d i", i=PACK))
+        nc.scalar.dma_start(gate_rows[P - 4 : P, :, :], gate[:, 0, :].rearrange("d (b v) -> b d v", b=4))
         nc.sync.dma_start(w_raw[:], w1.rearrange("(p j) n -> p j n", j=PACK))
-        nc.sync.dma_start(lists[0][:], cen)
+        nc.sync.dma_start(lists[0][:], pos1)
         nc.sync.dma_start(words[:].bitcast(I32), x_words[0].rearrange("p n t -> p (n t)").bitcast(I32))
-        nc.sync.dma_start(lists[1][:], pos1)
-        nc.sync.dma_start(lists[2][:], pos2)
-        nc.sync.dma_start(lists[3][:], pos3)
+        nc.sync.dma_start(lists[1][:], pos2)
+        nc.sync.dma_start(lists[2][:], pos3)
+        nc.sync.dma_start(lists[3][:], cen)
 
         make_identity(nc, ident[:])
+        gate_cols = bank(7, "gate_cols")
+        for d in range(D):
+            nc.tensor.transpose(gate_cols[:, d * P : (d + 1) * P], gate_rows[:, d, :], ident[:])
+        nc.scalar.copy(coef_t[:, 0:D, :], gate_cols[:].rearrange("p (d r) -> p d r", r=P)[:, 0:D, P - 4 : P])
         gsum = keep.tile([P, 2, PACK], F32, name="gsum")
-        nc.gpsimd.tensor_tensor(gsum[:, 0, :], coef_t[:, 1, 0:PACK], coef_t[:, 2, 0:PACK], ALU.add)
-        nc.gpsimd.tensor_tensor(gsum[:, 1, :], gsum[:, 0, :], coef_t[:, 3, 0:PACK], ALU.add)
-        nc.gpsimd.tensor_scalar(coef_t[:, 0, 0:PACK], gsum[:, 1, :], -1.0, 1.0, ALU.mult, ALU.add)
+        nc.gpsimd.tensor_tensor(gsum[:, 0, :], coef_t[:, 0, :], coef_t[:, 1, :], ALU.add)
+        nc.gpsimd.tensor_tensor(gsum[:, 1, :], gsum[:, 0, :], coef_t[:, 2, :], ALU.add)
+        nc.gpsimd.tensor_scalar(coef_t[:, D, :], gsum[:, 1, :], -1.0, 1.0, ALU.mult, ALU.add)
 
         w_codes = [keep.tile([P, P], U32, name=f"w_codes{m}", align_bytes=64) for m in range(2)]
         w_scales = [keep.tile([P, P], U8, name=f"w_scales{m}", align_bytes=64) for m in range(2)]
@@ -74,11 +80,11 @@ def tile_picked_grand_none_p_kernel(tc, x_words, x_scales, w1, gate, offs, cen, 
             quantize_w(m)
 
         coef = [keep.tile([P, V], F32, name=f"coef{d}") for d in range(D + 1)]
-        for d in (1, 2, 3, 0):
+        for d in range(D + 1):
             spread = bank(d, f"spread{d}")
             for i in range(PACK):
                 nc.tensor.transpose(spread[:, i * P : (i + 1) * P], coef_t[:, d, i : i + 1].to_broadcast([P, P]), ident[:])
-            nc.scalar.copy(coef[d][:].rearrange("q (p i) -> q p i", i=PACK), spread[:].rearrange("q (i p) -> q p i", i=PACK))
+            nc.scalar.copy(coef[d][:], spread[:])
 
         picked = [keep.tile([P, HALF], U32, name=f"picked{h}", align_bytes=64) for h in range(2)]
         y = [keep.tile([P, S], F32, name=f"y{m}") for m in range(2)]
@@ -100,14 +106,17 @@ def tile_picked_grand_none_p_kernel(tc, x_words, x_scales, w1, gate, offs, cen, 
         for h in range(2):
             nc.vector.tensor_copy(picked[h][:], words[:].indirect(offs_sb[:, h * HALF // 16 : (h + 1) * HALF // 16]))
         project(0, 4, 0, 512, nc.scalar.copy)
+        project(1, 7, 0, 512, nc.scalar.copy)
         project(0, 5, 512, 768, nc.vector.tensor_copy)
         project(0, 6, 768, 1024, nc.scalar.copy)
-        project(1, 7, 0, 512, nc.scalar.copy)
         project(1, 0, 512, 1024, nc.scalar.copy)
 
         terms = [[keep.tile([P, V], F32, name=f"term{m}_{d}") for d in range(D)] for m in range(2)]
-        terms[0].append(terms[1][1])
-        terms[1].append(terms[1][2])
+        last_terms = {(0, 0): terms[0][0], (0, 1): terms[1][1], (1, 0): terms[1][2], (1, 1): terms[1][2]}
+
+        def term(m, d, lo, hi):
+            return (terms[m][d] if d < D else last_terms[m, 2 * lo // V])[:, lo:hi]
+
         sum_banks = ((1, 2, 3, 4), (5, 6, 7, 0))
         sums = [[None] * 4, [None] * 4]
         turned = [keep.tile([P, V], F32, name=f"turned{m}") for m in range(2)]
@@ -115,14 +124,14 @@ def tile_picked_grand_none_p_kernel(tc, x_words, x_scales, w1, gate, offs, cen, 
         H = V // 2
 
         def fetch(m, d, lo, hi):
-            nc.vector.tensor_tensor(terms[m][d][:, lo:hi], y[m][:].indirect(lists[d][:, lo // 16 : hi // 16]), coef[d][:, lo:hi], ALU.mult)
+            nc.vector.tensor_tensor(term(m, d, lo, hi), y[m][:].indirect(lists[d][:, lo // 16 : hi // 16]), coef[d][:, lo:hi], ALU.mult)
 
         def add_up(m, d, blocks):
             for b in blocks:
                 if d == 0:
                     sums[m][b] = bank(sum_banks[m][b], f"sum{m}_{b}")
                 last = D if (m == 0 and b < 2) else D - 1
-                nc.tensor.matmul(sums[m][b][:, 0:P], terms[m][d][:, b * P : (b + 1) * P], ident[:], start=(d == 0), stop=(d == last), is_transpose=True)
+                nc.tensor.matmul(sums[m][b][:, 0:P], term(m, d, b * P, (b + 1) * P), ident[:], start=(d == 0), stop=(d == last), is_transpose=True)
 
         def turn_back(m, h):
             for b in (2 * h, 2 * h + 1):
@@ -132,28 +141,29 @@ def tile_picked_grand_none_p_kernel(tc, x_words, x_scales, w1, gate, offs, cen, 
                 nc.tensor.transpose(back[:, b * P : (b + 1) * P], turned[m][:, (2 * h + b) * P : (2 * h + b + 1) * P], ident[:])
             return back
 
-        def finish(m, h):
+        def finish(m, h, queue):
             cols = slice(h * H, (h + 1) * H)
-            nc.vector.tensor_tensor(res[m][:, cols], backs[m, h][:, 0:H], terms[m][D][:, cols], ALU.add)
-            nc.sync.dma_start(out[m * P : (m + 1) * P, cols], res[m][:, cols])
+            nc.vector.tensor_tensor(res[m][:, cols], backs[m, h][:, 0:H], term(m, D, h * H, (h + 1) * H), ALU.add)
+            queue.dma_start(out[m * P : (m + 1) * P, cols], res[m][:, cols])
 
         backs = {}
-        for m in range(2):
-            for d in range(D):
-                fetch(m, d, 0, V)
-                add_up(m, d, range(4))
-            if m == 0:
-                backs[0, 1] = turn_back(0, 1)
-        backs[1, 0] = turn_back(1, 0)
-        backs[1, 1] = turn_back(1, 1)
+        for d in range(D):
+            fetch(0, d, 0, V)
+            add_up(0, d, range(4))
         fetch(0, D, 0, H)
         add_up(0, D, range(2))
+        backs[0, 1] = turn_back(0, 1)
         backs[0, 0] = turn_back(0, 0)
         nc.scalar.copy(res[0][:, 0:H], backs[0, 0][:, 0:H])
-        nc.scalar.dma_start(out[0:P, 0:H], res[0][:, 0:H])
+        nc.sync.dma_start(out[0:P, 0:H], res[0][:, 0:H])
+        for d in range(D):
+            fetch(1, d, 0, V)
+            add_up(1, d, range(4))
+        backs[1, 0] = turn_back(1, 0)
+        backs[1, 1] = turn_back(1, 1)
         fetch(0, D, H, V)
         fetch(1, D, 0, H)
-        finish(0, 1)
+        finish(0, 1, nc.sync)
         fetch(1, D, H, V)
-        finish(1, 0)
-        finish(1, 1)
+        finish(1, 0, nc.sync)
+        finish(1, 1, nc.scalar)

@@ -17,6 +17,7 @@ U16 = mybir.dt.uint16
 U8 = mybir.dt.uint8
 FP8X4 = mybir.dt.float8_e4m3fn_x4
 ALU = mybir.AluOpType
+COPY = mybir.ActivationFunctionType.Copy
 
 
 def tile_picked_grand_none_p_kernel(tc, x_words, x_scales, w1, gate, offs, cen, pos1, pos2, pos3, out):
@@ -55,7 +56,7 @@ def tile_picked_grand_none_p_kernel(tc, x_words, x_scales, w1, gate, offs, cen, 
         gate_cols = bank(7, "gate_cols")
         for d in range(D):
             nc.tensor.transpose(gate_cols[:, d * P : (d + 1) * P], gate_rows[:, d, :], ident[:])
-        nc.scalar.copy(coef_t[:, 0:D, :], gate_cols[:].rearrange("p (d r) -> p d r", r=P)[:, 0:D, P - 4 : P])
+        nc.scalar.activation(coef_t[:, 0:D, :], gate_cols[:].rearrange("p (d r) -> p d r", r=P)[:, 0:D, P - 4 : P], COPY)
         gsum = keep.tile([P, 2, PACK], F32, name="gsum")
         nc.gpsimd.tensor_tensor(gsum[:, 0, :], coef_t[:, 0, :], coef_t[:, 1, :], ALU.add)
         nc.gpsimd.tensor_tensor(gsum[:, 1, :], gsum[:, 0, :], coef_t[:, 2, :], ALU.add)
@@ -105,65 +106,58 @@ def tile_picked_grand_none_p_kernel(tc, x_words, x_scales, w1, gate, offs, cen, 
 
         for h in range(2):
             nc.vector.tensor_copy(picked[h][:], words[:].indirect(offs_sb[:, h * HALF // 16 : (h + 1) * HALF // 16]))
-        project(0, 4, 0, 512, nc.scalar.copy)
-        project(1, 7, 0, 512, nc.scalar.copy)
-        project(0, 5, 512, 768, nc.vector.tensor_copy)
-        project(0, 6, 768, 1024, nc.scalar.copy)
-        project(1, 0, 512, 1024, nc.scalar.copy)
+        project(0, 0, 0, 512, nc.scalar.copy)
+        project(1, 1, 0, 512, nc.scalar.copy)
+        project(0, 2, 512, 768, nc.vector.tensor_copy)
+        project(0, 3, 768, 1024, nc.scalar.copy)
+        project(1, 4, 512, 1024, nc.scalar.copy)
 
-        terms = [[keep.tile([P, V], F32, name=f"term{m}_{d}") for d in range(D)] for m in range(2)]
-        last_terms = {(0, 0): terms[0][0], (0, 1): terms[1][1], (1, 0): terms[1][2], (1, 1): terms[1][2]}
-
-        def term(m, d, lo, hi):
-            return (terms[m][d] if d < D else last_terms[m, 2 * lo // V])[:, lo:hi]
-
-        sum_banks = ((1, 2, 3, 4), (5, 6, 7, 0))
-        sums = [[None] * 4, [None] * 4]
-        turned = [keep.tile([P, V], F32, name=f"turned{m}") for m in range(2)]
-        res = [keep.tile([P, V], F32, name=f"res{m}") for m in range(2)]
         H = V // 2
+        scaled = [keep.tile([P, V], F32, name=f"scaled{d}") for d in range(D + 1)]
+        partial = [keep.tile([P, V], F32, name=f"partial{d}") for d in range(2)]
+        centre1 = keep.tile([P, V], F32, name="centre1")
+        raw = [keep.tile([P, V], F32, name=f"raw{d}") for d in range(D)]
+        weighted = [keep.tile([P, V], F32, name=f"weighted{d}") for d in range(D)]
+        res = [keep.tile([P, V], F32, name=f"res{m}") for m in range(2)]
+        raw_t = [bank(b, f"raw_t{d}") for d, b in enumerate((6, 7, 0))]
+        back = [bank(1 + h, f"back{h}") for h in range(2)]
 
-        def fetch(m, d, lo, hi):
-            nc.vector.tensor_tensor(term(m, d, lo, hi), y[m][:].indirect(lists[d][:, lo // 16 : hi // 16]), coef[d][:, lo:hi], ALU.mult)
+        def block(b):
+            return slice(b * P, (b + 1) * P)
 
-        def add_up(m, d, blocks):
-            for b in blocks:
-                if d == 0:
-                    sums[m][b] = bank(sum_banks[m][b], f"sum{m}_{b}")
-                last = D if (m == 0 and b < 2) else D - 1
-                nc.tensor.matmul(sums[m][b][:, 0:P], term(m, d, b * P, (b + 1) * P), ident[:], start=(d == 0), stop=(d == last), is_transpose=True)
+        def fetch_scaled(dst, m, d):
+            nc.vector.tensor_tensor(dst[:], y[m][:].indirect(lists[d][:]), coef[d][:], ALU.mult)
 
-        def turn_back(m, h):
-            for b in (2 * h, 2 * h + 1):
-                nc.scalar.copy(turned[m][:, b * P : (b + 1) * P], sums[m][b][:, 0:P])
-            back = bank(sum_banks[m][2 * h], f"back{m}_{h}")
-            for b in range(2):
-                nc.tensor.transpose(back[:, b * P : (b + 1) * P], turned[m][:, (2 * h + b) * P : (2 * h + b + 1) * P], ident[:])
-            return back
+        def fetch_raw(d):
+            nc.scalar.activation(raw[d][:], y[1][:].indirect(lists[d][:]), COPY)
+            for b in range(4):
+                nc.tensor.transpose(raw_t[d][:, block(b)], raw[d][:, block(b)], ident[:])
 
-        def finish(m, h, queue):
+        def weigh(d):
+            for b in range(4):
+                nc.scalar.activation(weighted[d][:, block(b)], raw_t[d][:, block(b)], COPY, scale=coef_t[:, d, b : b + 1])
+            for b in range(4):
+                nc.tensor.matmul(back[b // 2][:, block(b % 2)], weighted[d][:, block(b)], ident[:], start=(d == 0 and b % 2 == 0), stop=(d == D - 1 and b % 2 == 1), is_transpose=True)
+
+        def finish(h, queue):
             cols = slice(h * H, (h + 1) * H)
-            nc.vector.tensor_tensor(res[m][:, cols], backs[m, h][:, 0:H], term(m, D, h * H, (h + 1) * H), ALU.add)
-            queue.dma_start(out[m * P : (m + 1) * P, cols], res[m][:, cols])
+            nc.vector.tensor_tensor(res[1][:, cols], back[h][:, 0:H], centre1[:, cols], ALU.add)
+            queue.dma_start(out[P : 2 * P, cols], res[1][:, cols])
 
-        backs = {}
-        for d in range(D):
-            fetch(0, d, 0, V)
-            add_up(0, d, range(4))
-        fetch(0, D, 0, H)
-        add_up(0, D, range(2))
-        backs[0, 1] = turn_back(0, 1)
-        backs[0, 0] = turn_back(0, 0)
-        nc.scalar.copy(res[0][:, 0:H], backs[0, 0][:, 0:H])
-        nc.sync.dma_start(out[0:P, 0:H], res[0][:, 0:H])
-        for d in range(D):
-            fetch(1, d, 0, V)
-            add_up(1, d, range(4))
-        backs[1, 0] = turn_back(1, 0)
-        backs[1, 1] = turn_back(1, 1)
-        fetch(0, D, H, V)
-        fetch(1, D, 0, H)
-        finish(0, 1, nc.sync)
-        fetch(1, D, H, V)
-        finish(1, 0, nc.sync)
-        finish(1, 1, nc.scalar)
+        fetch_scaled(scaled[0], 0, 0)
+        fetch_raw(0)
+        fetch_scaled(scaled[1], 0, 1)
+        fetch_raw(1)
+        fetch_scaled(scaled[2], 0, 2)
+        nc.vector.tensor_tensor(partial[0][:], scaled[0][:], scaled[1][:], ALU.add)
+        weigh(0)
+        fetch_raw(2)
+        fetch_scaled(scaled[D], 0, D)
+        nc.vector.tensor_tensor(partial[1][:], partial[0][:], scaled[2][:], ALU.add)
+        fetch_scaled(centre1, 1, D)
+        nc.vector.tensor_tensor(res[0][:], partial[1][:], scaled[D][:], ALU.add)
+        nc.sync.dma_start(out[0:P, :], res[0][:])
+        weigh(1)
+        weigh(2)
+        finish(0, nc.sync)
+        finish(1, nc.sync)

@@ -106,21 +106,23 @@ def tile_picked_grand_none_p_kernel(tc, x_words, x_scales, w1, gate, offs, cen, 
 
         for h in range(2):
             nc.vector.tensor_copy(picked[h][:], words[:].indirect(offs_sb[:, h * HALF // 16 : (h + 1) * HALF // 16]))
-        project(0, 0, 0, 512, nc.scalar.copy)
-        project(1, 1, 0, 512, nc.scalar.copy)
-        project(0, 2, 512, 768, nc.vector.tensor_copy)
-        project(0, 3, 768, 1024, nc.scalar.copy)
-        project(1, 4, 512, 1024, nc.scalar.copy)
+        Q = S // 4
+        for h in range(2):
+            for m in range(2):
+                for q in range(2):
+                    lo = h * HALF + q * Q
+                    on_vector = h == 1 and m == 0 and q == 0
+                    project(m, 4 * h + 2 * m + q, lo, lo + Q, nc.vector.tensor_copy if on_vector else nc.scalar.copy)
 
         H = V // 2
         scaled = [keep.tile([P, V], F32, name=f"scaled{d}") for d in range(D + 1)]
         partial = [keep.tile([P, V], F32, name=f"partial{d}") for d in range(2)]
         centre1 = keep.tile([P, V], F32, name="centre1")
-        raw = [keep.tile([P, V], F32, name=f"raw{d}") for d in range(D)]
+        raw = [keep.tile([P, V], F32, name=f"raw{d}") for d in range(2)]
         weighted = [keep.tile([P, V], F32, name=f"weighted{d}") for d in range(D)]
         res = [keep.tile([P, V], F32, name=f"res{m}") for m in range(2)]
-        raw_t = [bank(b, f"raw_t{d}") for d, b in enumerate((6, 7, 0))]
-        back = [bank(1 + h, f"back{h}") for h in range(2)]
+        raw_t = [bank(b, f"raw_t{b}") for b in range(4)]
+        back = [bank(4 + h, f"back{h}") for h in range(2)]
 
         def block(b):
             return slice(b * P, (b + 1) * P)
@@ -128,15 +130,20 @@ def tile_picked_grand_none_p_kernel(tc, x_words, x_scales, w1, gate, offs, cen, 
         def fetch_scaled(dst, m, d):
             nc.vector.tensor_tensor(dst[:], y[m][:].indirect(lists[d][:]), coef[d][:], ALU.mult)
 
-        def fetch_raw(d):
-            nc.scalar.activation(raw[d][:], y[1][:].indirect(lists[d][:]), COPY)
-            for b in range(4):
-                nc.tensor.transpose(raw_t[d][:, block(b)], raw[d][:, block(b)], ident[:])
+        def turned(d, b):
+            return raw_t[d if d < 2 else 2 + b // 2][:, block(b)]
 
-        def weigh(d):
-            for b in range(4):
-                nc.scalar.activation(weighted[d][:, block(b)], raw_t[d][:, block(b)], COPY, scale=coef_t[:, d, b : b + 1])
-            for b in range(4):
+        def fetch_raw(d, blocks):
+            lo, hi = blocks[0] * P, (blocks[-1] + 1) * P
+            dst = raw[min(d, 1)]
+            nc.scalar.activation(dst[:, lo:hi], y[1][:].indirect(lists[d][:, lo // 16 : hi // 16]), COPY)
+            for b in blocks:
+                nc.tensor.transpose(turned(d, b), dst[:, block(b)], ident[:])
+
+        def weigh(d, blocks):
+            for b in blocks:
+                nc.scalar.activation(weighted[d][:, block(b)], turned(d, b), COPY, scale=coef_t[:, d, b : b + 1])
+            for b in blocks:
                 nc.tensor.matmul(back[b // 2][:, block(b % 2)], weighted[d][:, block(b)], ident[:], start=(d == 0 and b % 2 == 0), stop=(d == D - 1 and b % 2 == 1), is_transpose=True)
 
         def finish(h, queue):
@@ -145,19 +152,24 @@ def tile_picked_grand_none_p_kernel(tc, x_words, x_scales, w1, gate, offs, cen, 
             queue.dma_start(out[P : 2 * P, cols], res[1][:, cols])
 
         fetch_scaled(scaled[0], 0, 0)
-        fetch_raw(0)
+        fetch_raw(0, (0, 1, 2, 3))
         fetch_scaled(scaled[1], 0, 1)
-        fetch_raw(1)
+        fetch_raw(1, (0, 1, 2, 3))
         fetch_scaled(scaled[2], 0, 2)
         nc.vector.tensor_tensor(partial[0][:], scaled[0][:], scaled[1][:], ALU.add)
-        weigh(0)
-        fetch_raw(2)
+        weigh(0, (0, 1, 2, 3))
+        fetch_raw(2, (0, 1))
         fetch_scaled(scaled[D], 0, D)
         nc.vector.tensor_tensor(partial[1][:], partial[0][:], scaled[2][:], ALU.add)
+        weigh(1, (0, 1))
+        fetch_raw(2, (2, 3))
         fetch_scaled(centre1, 1, D)
-        nc.vector.tensor_tensor(res[0][:], partial[1][:], scaled[D][:], ALU.add)
-        nc.sync.dma_start(out[0:P, :], res[0][:])
-        weigh(1)
-        weigh(2)
+        for h in range(2):
+            cols = slice(h * H, (h + 1) * H)
+            nc.vector.tensor_tensor(res[0][:, cols], partial[1][:, cols], scaled[D][:, cols], ALU.add)
+            nc.sync.dma_start(out[0:P, cols], res[0][:, cols])
+        weigh(1, (2, 3))
+        weigh(2, (0, 1))
+        weigh(2, (2, 3))
         finish(0, nc.sync)
         finish(1, nc.sync)

@@ -34,23 +34,25 @@ def tile_picked_grand_none_p_kernel(tc, x_words, x_scales, w1, gate, offs, cen, 
         words = keep.tile([P, T], U32, name="words", align_bytes=64)
         scales = keep.tile([P, T], U8, name="scales", align_bytes=64)
         planes = keep.tile([P, S], U8, name="planes", align_bytes=64)
-        w_raw = keep.tile([P, PACK, N], F32, name="w_raw")
+        w_raw = [keep.tile([P, PACK, P], F32, name=f"w_raw{m}", tag=f"w_raw{m}", align_bytes=64) for m in range(2)]
         gate_rows = keep.tile([P, D, P], F32, name="gate_rows")
-        coef_t = keep.tile([P, D + 1, 4], F32, name="coef_t")
+        coef_t = keep.tile([P, D, 4], F32, name="coef_t")
+        centre_t = keep.tile([P, 4], F32, name="centre_t", tag="w_bf", align_bytes=64)
         ident = keep.tile([P, P], F32, name="ident")
 
         nc.vector.memset(scales[0:112, :].bitcast(I32), 0)
         nc.vector.memset(gate_rows[0 : P - 4, :, :], 0.0)
         nc.vector.memset(planes[:].bitcast(I32), 0)
         nc.sync.dma_start(offs_sb[:], offs)
-        nc.sync.dma_start(scales[112:P, :].bitcast(I32), x_scales[0].bitcast(I32))
+        nc.scalar.dma_start(scales[112:P, :].bitcast(I32), x_scales[0].bitcast(I32))
         nc.scalar.dma_start(gate_rows[P - 4 : P, :, :], gate[:, 0, :].rearrange("d (b v) -> b d v", b=4))
-        nc.sync.dma_start(w_raw[:], w1.rearrange("(p j) n -> p j n", j=PACK))
-        nc.sync.dma_start(lists[0][:], pos1)
+        for d, places in enumerate((pos1, pos2, pos3)):
+            nc.sync.dma_start(lists[d][:], places)
         nc.sync.dma_start(words[:].bitcast(I32), x_words[0].rearrange("p n t -> p (n t)").bitcast(I32))
-        nc.sync.dma_start(lists[1][:], pos2)
-        nc.sync.dma_start(lists[2][:], pos3)
-        nc.sync.dma_start(lists[3][:], cen)
+        w_rows = w1.rearrange("(p j) n -> p j n", j=PACK)
+        for m in range(2):
+            nc.sync.dma_start(w_raw[m][:], w_rows[:, :, m * P : (m + 1) * P])
+        nc.sync.dma_start(lists[D][:], cen)
 
         make_identity(nc, ident[:])
         gate_cols = bank(7, "gate_cols")
@@ -60,34 +62,32 @@ def tile_picked_grand_none_p_kernel(tc, x_words, x_scales, w1, gate, offs, cen, 
         gsum = keep.tile([P, 2, PACK], F32, name="gsum")
         nc.gpsimd.tensor_tensor(gsum[:, 0, :], coef_t[:, 0, :], coef_t[:, 1, :], ALU.add)
         nc.gpsimd.tensor_tensor(gsum[:, 1, :], gsum[:, 0, :], coef_t[:, 2, :], ALU.add)
-        nc.gpsimd.tensor_scalar(coef_t[:, D, :], gsum[:, 1, :], -1.0, 1.0, ALU.mult, ALU.add)
+        nc.gpsimd.tensor_scalar(centre_t[:], gsum[:, 1, :], -1.0, 1.0, ALU.mult, ALU.add)
 
         w_codes = [keep.tile([P, P], U32, name=f"w_codes{m}", align_bytes=64) for m in range(2)]
         w_scales = [keep.tile([P, P], U8, name=f"w_scales{m}", align_bytes=64) for m in range(2)]
-        w_bf = [keep.tile([P, P, PACK], BF16, name=f"w_bf{m}", align_bytes=64) for m in range(2)]
 
         def round_w(m):
-            nc.scalar.copy(w_bf[m][:], w_raw[:, :, m * P : (m + 1) * P].rearrange("p j n -> p n j"))
+            nc.scalar.copy(w_bf[m], w_raw[m][:].rearrange("p j n -> p n j"))
 
         def quantize_w(m):
-            nc.vector.quantize_mx(out=w_codes[m][:].bitcast(FP8X4), scales=w_scales[m][:], in_=w_bf[m][:].rearrange("p n j -> p (n j)"))
+            nc.vector.quantize_mx(out=w_codes[m][:].bitcast(FP8X4), scales=w_scales[m][:], in_=w_bf[m].rearrange("p n j -> p (n j)"))
 
         picked_scales = keep.tile([P, S], U8, name="picked_scales", align_bytes=64)
         nc.vector.tensor_copy(picked_scales[:], scales[:].indirect(offs_sb[:]))
         for i in range(4):
             nc.sync.dma_start(planes[i:P:32, :].bitcast(I32), picked_scales[112 + i : P : 4, :].bitcast(I32))
-        for m in range(2):
-            round_w(m)
-            quantize_w(m)
 
         coef = [keep.tile([P, V], F32, name=f"coef{d}") for d in range(D + 1)]
         for d in range(D + 1):
             spread = bank(d, f"spread{d}")
             for i in range(PACK):
-                nc.tensor.transpose(spread[:, i * P : (i + 1) * P], coef_t[:, d, i : i + 1].to_broadcast([P, P]), ident[:])
+                nc.tensor.transpose(spread[:, i * P : (i + 1) * P], (coef_t[:, d, :] if d < D else centre_t[:])[:, i : i + 1].to_broadcast([P, P]), ident[:])
             nc.scalar.copy(coef[d][:], spread[:])
 
-        picked = [keep.tile([P, HALF], U32, name=f"picked{h}", align_bytes=64) for h in range(2)]
+        w_both = keep.tile([P, 2, P, PACK], BF16, name="w_both", tag="w_bf", align_bytes=64)
+        w_bf = [w_both[:, m] for m in range(2)]
+        picked = []
         y = [keep.tile([P, S], F32, name=f"y{m}") for m in range(2)]
 
         def project(m, b, lo, hi, engine_copy):
@@ -104,15 +104,16 @@ def tile_picked_grand_none_p_kernel(tc, x_words, x_scales, w1, gate, offs, cen, 
             )
             engine_copy(y[m][:, lo:hi], acc[:, 0 : hi - lo])
 
-        for h in range(2):
+        for h, tag in enumerate(("picked0", "w_raw0")):
+            picked.append(keep.tile([P, HALF], U32, name=f"picked{h}", tag=tag, align_bytes=64))
             nc.vector.tensor_copy(picked[h][:], words[:].indirect(offs_sb[:, h * HALF // 16 : (h + 1) * HALF // 16]))
-        Q = S // 4
-        for h in range(2):
-            for m in range(2):
-                for q in range(2):
-                    lo = h * HALF + q * Q
-                    on_vector = h == 1 and m == 0 and q == 0
-                    project(m, 4 * h + 2 * m + q, lo, lo + Q, nc.vector.tensor_copy if on_vector else nc.scalar.copy)
+            round_w(h)
+            quantize_w(h)
+        project(0, 0, 0, 512, nc.scalar.copy)
+        project(0, 2, 512, 768, nc.vector.tensor_copy)
+        project(0, 3, 768, 1024, nc.scalar.copy)
+        project(1, 1, 0, 512, nc.scalar.copy)
+        project(1, 4, 512, 1024, nc.scalar.copy)
 
         H = V // 2
         scaled = [keep.tile([P, V], F32, name=f"scaled{d}") for d in range(D + 1)]
@@ -121,8 +122,8 @@ def tile_picked_grand_none_p_kernel(tc, x_words, x_scales, w1, gate, offs, cen, 
         raw = [keep.tile([P, V], F32, name=f"raw{d}") for d in range(2)]
         weighted = [keep.tile([P, V], F32, name=f"weighted{d}") for d in range(D)]
         res = [keep.tile([P, V], F32, name=f"res{m}") for m in range(2)]
-        raw_t = [bank(b, f"raw_t{b}") for b in range(4)]
-        back = [bank(4 + h, f"back{h}") for h in range(2)]
+        raw_t = [bank(b, f"raw_t{i}") for i, b in enumerate((5, 6, 7, 0))]
+        back = [bank(2 + h, f"back{h}") for h in range(2)]
 
         def block(b):
             return slice(b * P, (b + 1) * P)

@@ -36,7 +36,9 @@ def tile_picked_grand_none_p_kernel(tc, x_words, x_scales, w1, gate, offs, cen, 
         planes = keep.tile([P, S], U8, name="planes", align_bytes=64)
         w_raw = [keep.tile([P, PACK, P], F32, name=f"w_raw{m}", tag=f"w_raw{m}", align_bytes=64) for m in range(2)]
         gate_rows = keep.tile([P, D, P], F32, name="gate_rows")
-        coef_t = keep.tile([P, D, 4], F32, name="coef_t")
+        first_t = keep.tile([P, 4], F32, name="first_t", tag="first_t")
+        later_t = keep.tile([P, D - 1, 4], F32, name="later_t")
+        coef_t = [first_t[:], later_t[:, 0, :], later_t[:, 1, :]]
         centre_t = keep.tile([P, 4], F32, name="centre_t", tag="w_bf", align_bytes=64)
         ident = keep.tile([P, P], F32, name="ident")
 
@@ -46,26 +48,32 @@ def tile_picked_grand_none_p_kernel(tc, x_words, x_scales, w1, gate, offs, cen, 
         nc.sync.dma_start(offs_sb[:], offs)
         nc.scalar.dma_start(scales[112:P, :].bitcast(I32), x_scales[0].bitcast(I32))
         nc.scalar.dma_start(gate_rows[P - 4 : P, :, :], gate[:, 0, :].rearrange("d (b v) -> b d v", b=4))
-        for d, places in enumerate((pos1, pos2, pos3)):
-            nc.sync.dma_start(lists[d][:], places)
-        nc.sync.dma_start(words[:].bitcast(I32), x_words[0].rearrange("p n t -> p (n t)").bitcast(I32))
         w_rows = w1.rearrange("(p j) n -> p j n", j=PACK)
-        for m in range(2):
-            nc.sync.dma_start(w_raw[m][:], w_rows[:, :, m * P : (m + 1) * P])
+        nc.sync.dma_start(w_raw[0][:], w_rows[:, :, 0:P])
+        nc.sync.dma_start(lists[0][:], pos1)
+        nc.sync.dma_start(lists[1][:], pos2)
+        nc.sync.dma_start(words[:].bitcast(I32), x_words[0].rearrange("p n t -> p (n t)").bitcast(I32))
+        nc.sync.dma_start(w_raw[1][:], w_rows[:, :, P:N])
+        nc.sync.dma_start(lists[2][:], pos3)
         nc.sync.dma_start(lists[D][:], cen)
 
         make_identity(nc, ident[:])
         gate_cols = bank(7, "gate_cols")
         for d in range(D):
             nc.tensor.transpose(gate_cols[:, d * P : (d + 1) * P], gate_rows[:, d, :], ident[:])
-        nc.scalar.activation(coef_t[:, 0:D, :], gate_cols[:].rearrange("p (d r) -> p d r", r=P)[:, 0:D, P - 4 : P], COPY)
+        gate_view = gate_cols[:].rearrange("p (d r) -> p d r", r=P)
+        nc.scalar.activation(first_t[:], gate_view[:, 0, P - 4 : P], COPY)
+        nc.scalar.activation(later_t[:], gate_view[:, 1:D, P - 4 : P], COPY)
         gsum = keep.tile([P, 2, PACK], F32, name="gsum")
-        nc.gpsimd.tensor_tensor(gsum[:, 0, :], coef_t[:, 0, :], coef_t[:, 1, :], ALU.add)
-        nc.gpsimd.tensor_tensor(gsum[:, 1, :], gsum[:, 0, :], coef_t[:, 2, :], ALU.add)
+        nc.gpsimd.tensor_tensor(gsum[:, 0, :], coef_t[0], coef_t[1], ALU.add)
+        nc.gpsimd.tensor_tensor(gsum[:, 1, :], gsum[:, 0, :], coef_t[2], ALU.add)
         nc.gpsimd.tensor_scalar(centre_t[:], gsum[:, 1, :], -1.0, 1.0, ALU.mult, ALU.add)
 
         w_codes = [keep.tile([P, P], U32, name=f"w_codes{m}", align_bytes=64) for m in range(2)]
         w_scales = [keep.tile([P, P], U8, name=f"w_scales{m}", align_bytes=64) for m in range(2)]
+
+        w_bf0 = keep.tile([P, P, PACK], BF16, name="w_bf0", align_bytes=64)
+        w_bf = [w_bf0[:]]
 
         def round_w(m):
             nc.scalar.copy(w_bf[m], w_raw[m][:].rearrange("p j n -> p n j"))
@@ -78,16 +86,19 @@ def tile_picked_grand_none_p_kernel(tc, x_words, x_scales, w1, gate, offs, cen, 
         for i in range(4):
             nc.sync.dma_start(planes[i:P:32, :].bitcast(I32), picked_scales[112 + i : P : 4, :].bitcast(I32))
 
+        round_w(0)
+        quantize_w(0)
+
         coef = [keep.tile([P, V], F32, name=f"coef{d}") for d in range(D + 1)]
         for d in range(D + 1):
             spread = bank(d, f"spread{d}")
             for i in range(PACK):
-                nc.tensor.transpose(spread[:, i * P : (i + 1) * P], (coef_t[:, d, :] if d < D else centre_t[:])[:, i : i + 1].to_broadcast([P, P]), ident[:])
+                nc.tensor.transpose(spread[:, i * P : (i + 1) * P], (coef_t[d] if d < D else centre_t[:])[:, i : i + 1].to_broadcast([P, P]), ident[:])
             nc.scalar.copy(coef[d][:], spread[:])
 
-        w_both = keep.tile([P, 2, P, PACK], BF16, name="w_both", tag="w_bf", align_bytes=64)
-        w_bf = [w_both[:, m] for m in range(2)]
-        picked = []
+        w_bf1 = keep.tile([P, P, PACK], BF16, name="w_bf1", tag="w_bf", align_bytes=64)
+        w_bf.append(w_bf1[:])
+        picked = [keep.tile([P, HALF], U32, name=f"picked{h}", align_bytes=64) for h in range(2)]
         y = [keep.tile([P, S], F32, name=f"y{m}") for m in range(2)]
 
         def project(m, b, lo, hi, engine_copy):
@@ -104,11 +115,10 @@ def tile_picked_grand_none_p_kernel(tc, x_words, x_scales, w1, gate, offs, cen, 
             )
             engine_copy(y[m][:, lo:hi], acc[:, 0 : hi - lo])
 
-        for h, tag in enumerate(("picked0", "w_raw0")):
-            picked.append(keep.tile([P, HALF], U32, name=f"picked{h}", tag=tag, align_bytes=64))
+        for h in range(2):
             nc.vector.tensor_copy(picked[h][:], words[:].indirect(offs_sb[:, h * HALF // 16 : (h + 1) * HALF // 16]))
-            round_w(h)
-            quantize_w(h)
+        round_w(1)
+        quantize_w(1)
         project(0, 0, 0, 512, nc.scalar.copy)
         project(0, 2, 512, 768, nc.vector.tensor_copy)
         project(0, 3, 768, 1024, nc.scalar.copy)
@@ -116,13 +126,12 @@ def tile_picked_grand_none_p_kernel(tc, x_words, x_scales, w1, gate, offs, cen, 
         project(1, 4, 512, 1024, nc.scalar.copy)
 
         H = V // 2
-        scaled = [keep.tile([P, V], F32, name=f"scaled{d}") for d in range(D + 1)]
+        scaled = [keep.tile([P, V], F32, name=f"scaled{d}") for d in range(D)]
         partial = [keep.tile([P, V], F32, name=f"partial{d}") for d in range(2)]
-        centre1 = keep.tile([P, V], F32, name="centre1")
-        raw = [keep.tile([P, V], F32, name=f"raw{d}") for d in range(2)]
+        raw = [keep.tile([P, V], F32, name=f"raw{d}", tag=f"raw{d}") for d in range(D)]
         weighted = [keep.tile([P, V], F32, name=f"weighted{d}") for d in range(D)]
         res = [keep.tile([P, V], F32, name=f"res{m}") for m in range(2)]
-        raw_t = [bank(b, f"raw_t{i}") for i, b in enumerate((5, 6, 7, 0))]
+        raw_t = [bank(b, f"raw_t{i}") for i, b in enumerate((5, 1, 6, 7, 0))]
         back = [bank(2 + h, f"back{h}") for h in range(2)]
 
         def block(b):
@@ -132,18 +141,21 @@ def tile_picked_grand_none_p_kernel(tc, x_words, x_scales, w1, gate, offs, cen, 
             nc.vector.tensor_tensor(dst[:], y[m][:].indirect(lists[d][:]), coef[d][:], ALU.mult)
 
         def turned(d, b):
-            return raw_t[d if d < 2 else 2 + b // 2][:, block(b)]
+            return raw_t[(b // 2, 2, 3 + b // 2)[d]][:, block(b)]
 
         def fetch_raw(d, blocks):
             lo, hi = blocks[0] * P, (blocks[-1] + 1) * P
-            dst = raw[min(d, 1)]
+            dst = raw[d if lo == 0 else min(d, 1)]
             nc.scalar.activation(dst[:, lo:hi], y[1][:].indirect(lists[d][:, lo // 16 : hi // 16]), COPY)
             for b in blocks:
                 nc.tensor.transpose(turned(d, b), dst[:, block(b)], ident[:])
 
         def weigh(d, blocks):
             for b in blocks:
-                nc.scalar.activation(weighted[d][:, block(b)], turned(d, b), COPY, scale=coef_t[:, d, b : b + 1])
+                nc.scalar.activation(weighted[d][:, block(b)], turned(d, b), COPY, scale=coef_t[d][:, b : b + 1])
+            turn_back(d, blocks)
+
+        def turn_back(d, blocks):
             for b in blocks:
                 nc.tensor.matmul(back[b // 2][:, block(b % 2)], weighted[d][:, block(b)], ident[:], start=(d == 0 and b % 2 == 0), stop=(d == D - 1 and b % 2 == 1), is_transpose=True)
 
@@ -152,22 +164,32 @@ def tile_picked_grand_none_p_kernel(tc, x_words, x_scales, w1, gate, offs, cen, 
             nc.vector.tensor_tensor(res[1][:, cols], back[h][:, 0:H], centre1[:, cols], ALU.add)
             queue.dma_start(out[P : 2 * P, cols], res[1][:, cols])
 
+        halves = [slice(h * H, (h + 1) * H) for h in range(2)]
         fetch_scaled(scaled[0], 0, 0)
         fetch_raw(0, (0, 1, 2, 3))
         fetch_scaled(scaled[1], 0, 1)
         fetch_raw(1, (0, 1, 2, 3))
         fetch_scaled(scaled[2], 0, 2)
         nc.vector.tensor_tensor(partial[0][:], scaled[0][:], scaled[1][:], ALU.add)
-        weigh(0, (0, 1, 2, 3))
+        nc.vector.tensor_tensor(
+            weighted[0][:, 0:H].rearrange("p (b m) -> p b m", b=2),
+            raw_t[0][:, 0:H].rearrange("p (b m) -> p b m", b=2),
+            first_t[:, 0:2].unsqueeze(2).to_broadcast([P, 2, P]),
+            ALU.mult,
+        )
         fetch_raw(2, (0, 1))
-        fetch_scaled(scaled[D], 0, D)
-        nc.vector.tensor_tensor(partial[1][:], partial[0][:], scaled[2][:], ALU.add)
+        turn_back(0, (0, 1))
+        weigh(0, (2, 3))
+        centre0 = keep.tile([P, V], F32, name="centre0", tag="raw0")
+        fetch_scaled(centre0, 0, D)
+        centre1 = keep.tile([P, V], F32, name="centre1", tag="first_t")
+        fetch_scaled(centre1, 1, D)
         weigh(1, (0, 1))
         fetch_raw(2, (2, 3))
-        fetch_scaled(centre1, 1, D)
-        for h in range(2):
-            cols = slice(h * H, (h + 1) * H)
-            nc.vector.tensor_tensor(res[0][:, cols], partial[1][:, cols], scaled[D][:, cols], ALU.add)
+        for cols in halves:
+            nc.vector.tensor_tensor(partial[1][:, cols], partial[0][:, cols], centre0[:, cols], ALU.add)
+        for cols in halves:
+            nc.vector.tensor_tensor(res[0][:, cols], partial[1][:, cols], scaled[2][:, cols], ALU.add)
             nc.sync.dma_start(out[0:P, cols], res[0][:, cols])
         weigh(1, (2, 3))
         weigh(2, (0, 1))

@@ -6,7 +6,11 @@ from concourse.masks import make_identity
 K, T, S, D, V, N = 512, 4096, 1024, 3, 512, 256
 P = 128
 PACK = 4
-HALF = S // 2
+BLOCKS = V // P
+SCALE_ROWS = K // 32
+PER_COLUMN = 16
+HALF_S = S // 2
+HALF_V = V // 2
 FLOPS = 2 * K * N * S
 
 F32 = mybir.dt.float32
@@ -20,34 +24,38 @@ ALU = mybir.AluOpType
 COPY = mybir.ActivationFunctionType.Copy
 
 
+def block(b):
+    return slice(b * P, (b + 1) * P)
+
+
 def tile_picked_grand_none_p_kernel(tc, x_words, x_scales, w1, gate, offs, cen, pos1, pos2, pos3, out):
     nc = tc.nc
     with ExitStack() as ctx:
         keep = ctx.enter_context(tc.tile_pool(name="keep", bufs=1))
         psum = ctx.enter_context(tc.psum_pool(name="psum", bufs=1))
 
-        def bank(b, name):
-            return psum.tile([P, 512], F32, name=name, tag=f"bank{b}")
+        def bank(number, name):
+            return psum.tile([P, 512], F32, name=name, tag=f"bank{number}")
 
-        offs_sb = keep.tile([P, S // 16], U16, name="offs_sb")
-        lists = [keep.tile([P, V // 16], U16, name=f"list{d}") for d in range(D + 1)]
+        offs_sb = keep.tile([P, S // PER_COLUMN], U16, name="offs_sb")
+        lists = [keep.tile([P, V // PER_COLUMN], U16, name=f"list{d}") for d in range(D + 1)]
         words = keep.tile([P, T], U32, name="words", align_bytes=64)
         scales = keep.tile([P, T], U8, name="scales", align_bytes=64)
-        planes = keep.tile([P, S], U8, name="planes", align_bytes=64)
-        w_raw = [keep.tile([P, PACK, P], F32, name=f"w_raw{m}", tag=f"w_raw{m}", align_bytes=64) for m in range(2)]
+        plane = keep.tile([P, S], U8, name="plane", align_bytes=64)
+        w_raw = [keep.tile([P, PACK, P], F32, name=f"w_raw{m}", align_bytes=64) for m in range(2)]
         gate_rows = keep.tile([P, D, P], F32, name="gate_rows")
-        first_t = keep.tile([P, 4], F32, name="first_t", tag="first_t")
-        later_t = keep.tile([P, D - 1, 4], F32, name="later_t")
-        coef_t = [first_t[:], later_t[:, 0, :], later_t[:, 1, :]]
-        centre_t = keep.tile([P, 4], F32, name="centre_t", tag="w_bf", align_bytes=64)
+        gate_t = keep.tile([P, D, BLOCKS], F32, name="gate_t")
+        centre_t = keep.tile([P, BLOCKS], F32, name="centre_t", tag="centre_t_then_w_bf1", align_bytes=64)
         ident = keep.tile([P, P], F32, name="ident")
 
-        nc.vector.memset(scales[0:112, :].bitcast(I32), 0)
-        nc.vector.memset(gate_rows[0 : P - 4, :, :], 0.0)
-        nc.vector.memset(planes[:].bitcast(I32), 0)
+        first_scale_row = P - SCALE_ROWS
+        first_gate_row = P - BLOCKS
+        nc.vector.memset(scales[0:first_scale_row, :].bitcast(I32), 0)
+        nc.vector.memset(gate_rows[0:first_gate_row, :, :], 0.0)
+        nc.vector.memset(plane[:].bitcast(I32), 0)
         nc.sync.dma_start(offs_sb[:], offs)
-        nc.scalar.dma_start(scales[112:P, :].bitcast(I32), x_scales[0].bitcast(I32))
-        nc.scalar.dma_start(gate_rows[P - 4 : P, :, :], gate[:, 0, :].rearrange("d (b v) -> b d v", b=4))
+        nc.scalar.dma_start(scales[first_scale_row:P, :].bitcast(I32), x_scales[0].bitcast(I32))
+        nc.scalar.dma_start(gate_rows[first_gate_row:P, :, :], gate[:, 0, :].rearrange("d (b v) -> b d v", b=BLOCKS))
         w_rows = w1.rearrange("(p j) n -> p j n", j=PACK)
         nc.sync.dma_start(w_raw[0][:], w_rows[:, :, 0:P])
         nc.sync.dma_start(lists[0][:], pos1)
@@ -58,141 +66,127 @@ def tile_picked_grand_none_p_kernel(tc, x_words, x_scales, w1, gate, offs, cen, 
         nc.sync.dma_start(lists[D][:], cen)
 
         make_identity(nc, ident[:])
-        gate_cols = bank(7, "gate_cols")
+        gate_turned = bank(7, "gate_turned")
         for d in range(D):
-            nc.tensor.transpose(gate_cols[:, d * P : (d + 1) * P], gate_rows[:, d, :], ident[:])
-        gate_view = gate_cols[:].rearrange("p (d r) -> p d r", r=P)
-        nc.scalar.activation(first_t[:], gate_view[:, 0, P - 4 : P], COPY)
-        nc.scalar.activation(later_t[:], gate_view[:, 1:D, P - 4 : P], COPY)
-        gsum = keep.tile([P, 2, PACK], F32, name="gsum")
-        nc.gpsimd.tensor_tensor(gsum[:, 0, :], coef_t[0], coef_t[1], ALU.add)
-        nc.gpsimd.tensor_tensor(gsum[:, 1, :], gsum[:, 0, :], coef_t[2], ALU.add)
-        nc.gpsimd.tensor_scalar(centre_t[:], gsum[:, 1, :], -1.0, 1.0, ALU.mult, ALU.add)
+            nc.tensor.transpose(gate_turned[:, block(d)], gate_rows[:, d, :], ident[:])
+        nc.scalar.activation(gate_t[:], gate_turned[:].rearrange("p (d r) -> p d r", r=P)[:, 0:D, first_gate_row:P], COPY)
+        gate_sum = keep.tile([P, 2, BLOCKS], F32, name="gate_sum")
+        nc.gpsimd.tensor_tensor(gate_sum[:, 0, :], gate_t[:, 0, :], gate_t[:, 1, :], ALU.add)
+        nc.gpsimd.tensor_tensor(gate_sum[:, 1, :], gate_sum[:, 0, :], gate_t[:, 2, :], ALU.add)
+        nc.gpsimd.tensor_scalar(centre_t[:], gate_sum[:, 1, :], -1.0, 1.0, ALU.mult, ALU.add)
 
         w_codes = [keep.tile([P, P], U32, name=f"w_codes{m}", align_bytes=64) for m in range(2)]
         w_scales = [keep.tile([P, P], U8, name=f"w_scales{m}", align_bytes=64) for m in range(2)]
 
+        def quantize_w(m, w_bf):
+            nc.scalar.copy(w_bf[:], w_raw[m][:].rearrange("p j n -> p n j"))
+            nc.vector.quantize_mx(out=w_codes[m][:].bitcast(FP8X4), scales=w_scales[m][:], in_=w_bf[:].rearrange("p n j -> p (n j)"))
+
         w_bf0 = keep.tile([P, P, PACK], BF16, name="w_bf0", align_bytes=64)
-        w_bf = [w_bf0[:]]
-
-        def round_w(m):
-            nc.scalar.copy(w_bf[m], w_raw[m][:].rearrange("p j n -> p n j"))
-
-        def quantize_w(m):
-            nc.vector.quantize_mx(out=w_codes[m][:].bitcast(FP8X4), scales=w_scales[m][:], in_=w_bf[m].rearrange("p n j -> p (n j)"))
 
         picked_scales = keep.tile([P, S], U8, name="picked_scales", align_bytes=64)
         nc.vector.tensor_copy(picked_scales[:], scales[:].indirect(offs_sb[:]))
         for i in range(4):
-            nc.sync.dma_start(planes[i:P:32, :].bitcast(I32), picked_scales[112 + i : P : 4, :].bitcast(I32))
+            nc.sync.dma_start(plane[i:P:32, :].bitcast(I32), picked_scales[first_scale_row + i : P : 4, :].bitcast(I32))
 
-        round_w(0)
-        quantize_w(0)
+        quantize_w(0, w_bf0)
 
-        coef = [keep.tile([P, V], F32, name=f"coef{d}") for d in range(D + 1)]
+        factor = [keep.tile([P, V], F32, name=f"factor{d}") for d in range(D + 1)]
         for d in range(D + 1):
             spread = bank(d, f"spread{d}")
-            for i in range(PACK):
-                nc.tensor.transpose(spread[:, i * P : (i + 1) * P], (coef_t[d] if d < D else centre_t[:])[:, i : i + 1].to_broadcast([P, P]), ident[:])
-            nc.scalar.copy(coef[d][:], spread[:])
+            columns = gate_t[:, d, :] if d < D else centre_t[:]
+            for b in range(BLOCKS):
+                nc.tensor.transpose(spread[:, block(b)], columns[:, b : b + 1].to_broadcast([P, P]), ident[:])
+            nc.scalar.copy(factor[d][:], spread[:])
 
-        w_bf1 = keep.tile([P, P, PACK], BF16, name="w_bf1", tag="w_bf", align_bytes=64)
-        w_bf.append(w_bf1[:])
-        picked = [keep.tile([P, HALF], U32, name=f"picked{h}", align_bytes=64) for h in range(2)]
+        w_bf1 = keep.tile([P, P, PACK], BF16, name="w_bf1", tag="centre_t_then_w_bf1", align_bytes=64)
+
+        picked = [keep.tile([P, HALF_S], U32, name=f"picked{h}", align_bytes=64) for h in range(2)]
         y = [keep.tile([P, S], F32, name=f"y{m}") for m in range(2)]
 
-        def project(m, b, lo, hi, engine_copy):
-            h = lo // HALF
-            acc = bank(b, f"acc{m}_{lo}")
+        def project(m, number, lo, hi, copy_out):
+            h = lo // HALF_S
+            acc = bank(number, f"acc{m}_{lo}")
             nc.tensor.matmul_mx(
                 out=acc[:, 0 : hi - lo],
                 lhsT=w_codes[m][:].bitcast(FP8X4),
                 lhsT_scale=w_scales[m][:],
-                rhs=picked[h][:, lo - h * HALF : hi - h * HALF].bitcast(FP8X4),
-                rhs_scale=planes[:, lo:hi],
+                rhs=picked[h][:, lo - h * HALF_S : hi - h * HALF_S].bitcast(FP8X4),
+                rhs_scale=plane[:, lo:hi],
                 start=True,
                 stop=True,
             )
-            engine_copy(y[m][:, lo:hi], acc[:, 0 : hi - lo])
+            copy_out(y[m][:, lo:hi], acc[:, 0 : hi - lo])
 
         for h in range(2):
-            nc.vector.tensor_copy(picked[h][:], words[:].indirect(offs_sb[:, h * HALF // 16 : (h + 1) * HALF // 16]))
-        round_w(1)
-        quantize_w(1)
-        project(0, 0, 0, 512, nc.scalar.copy)
-        project(0, 2, 512, 768, nc.vector.tensor_copy)
-        project(0, 3, 768, 1024, nc.scalar.copy)
-        project(1, 1, 0, 512, nc.scalar.copy)
-        project(1, 4, 512, 1024, nc.scalar.copy)
+            entries = slice(h * HALF_S // PER_COLUMN, (h + 1) * HALF_S // PER_COLUMN)
+            nc.vector.tensor_copy(picked[h][:], words[:].indirect(offs_sb[:, entries]))
+        quantize_w(1, w_bf1)
+        three_quarters = HALF_S + HALF_S // 2
+        project(0, 0, 0, HALF_S, nc.scalar.copy)
+        project(0, 2, HALF_S, three_quarters, nc.vector.tensor_copy)
+        project(0, 3, three_quarters, S, nc.scalar.copy)
+        project(1, 1, 0, HALF_S, nc.scalar.copy)
+        project(1, 4, HALF_S, S, nc.scalar.copy)
 
-        H = V // 2
-        scaled = [keep.tile([P, V], F32, name=f"scaled{d}") for d in range(D)]
-        partial = [keep.tile([P, V], F32, name=f"partial{d}") for d in range(2)]
-        raw = [keep.tile([P, V], F32, name=f"raw{d}", tag=f"raw{d}") for d in range(D)]
+        term = [keep.tile([P, V], F32, name=f"term{d}") for d in range(D)]
+        partial = [keep.tile([P, V], F32, name=f"partial{i}") for i in range(2)]
+        raw = [keep.tile([P, V], F32, name=f"raw{d}") for d in range(D)]
         weighted = [keep.tile([P, V], F32, name=f"weighted{d}") for d in range(D)]
         res = [keep.tile([P, V], F32, name=f"res{m}") for m in range(2)]
-        raw_t = [bank(b, f"raw_t{i}") for i, b in enumerate((5, 1, 6, 7, 0))]
-        back = [bank(2 + h, f"back{h}") for h in range(2)]
-
-        def block(b):
-            return slice(b * P, (b + 1) * P)
+        turned_banks = [bank(number, f"turned{i}") for i, number in enumerate((5, 6, 7, 0))]
+        pieces = ((0, 1), (2,), (3,))
+        sums = [bank(2 + i, f"sum{i}") for i in range(len(pieces))]
+        centre = [keep.tile([P, V], F32, name=f"centre{m}") for m in range(2)]
 
         def fetch_scaled(dst, m, d):
-            nc.vector.tensor_tensor(dst[:], y[m][:].indirect(lists[d][:]), coef[d][:], ALU.mult)
+            nc.vector.tensor_tensor(dst[:], y[m][:].indirect(lists[d][:]), factor[d][:], ALU.mult)
 
         def turned(d, b):
-            return raw_t[(b // 2, 2, 3 + b // 2)[d]][:, block(b)]
+            return turned_banks[d if d < D - 1 else d + b // 2][:, block(b)]
 
-        def fetch_raw(d, blocks):
+        def fetch_raw(d, blocks, dst):
             lo, hi = blocks[0] * P, (blocks[-1] + 1) * P
-            dst = raw[d if lo == 0 else min(d, 1)]
-            nc.scalar.activation(dst[:, lo:hi], y[1][:].indirect(lists[d][:, lo // 16 : hi // 16]), COPY)
+            nc.scalar.activation(dst[:, lo:hi], y[1][:].indirect(lists[d][:, lo // PER_COLUMN : hi // PER_COLUMN]), COPY)
             for b in blocks:
                 nc.tensor.transpose(turned(d, b), dst[:, block(b)], ident[:])
 
         def weigh(d, blocks):
             for b in blocks:
-                nc.scalar.activation(weighted[d][:, block(b)], turned(d, b), COPY, scale=coef_t[d][:, b : b + 1])
-            turn_back(d, blocks)
-
-        def turn_back(d, blocks):
+                nc.scalar.activation(weighted[d][:, block(b)], turned(d, b), COPY, scale=gate_t[:, d, b : b + 1])
             for b in blocks:
-                nc.tensor.matmul(back[b // 2][:, block(b % 2)], weighted[d][:, block(b)], ident[:], start=(d == 0 and b % 2 == 0), stop=(d == D - 1 and b % 2 == 1), is_transpose=True)
+                i = max(b - 1, 0)
+                first, last = pieces[i][0], pieces[i][-1]
+                nc.tensor.matmul(
+                    sums[i][:, block(b - first)],
+                    weighted[d][:, block(b)],
+                    ident[:],
+                    start=(d == 0 and b == first),
+                    stop=(d == D - 1 and b == last),
+                    is_transpose=True,
+                )
 
-        def finish(h, queue):
-            cols = slice(h * H, (h + 1) * H)
-            nc.vector.tensor_tensor(res[1][:, cols], back[h][:, 0:H], centre1[:, cols], ALU.add)
-            queue.dma_start(out[P : 2 * P, cols], res[1][:, cols])
-
-        halves = [slice(h * H, (h + 1) * H) for h in range(2)]
-        fetch_scaled(scaled[0], 0, 0)
-        fetch_raw(0, (0, 1, 2, 3))
-        fetch_scaled(scaled[1], 0, 1)
-        fetch_raw(1, (0, 1, 2, 3))
-        fetch_scaled(scaled[2], 0, 2)
-        nc.vector.tensor_tensor(partial[0][:], scaled[0][:], scaled[1][:], ALU.add)
-        nc.vector.tensor_tensor(
-            weighted[0][:, 0:H].rearrange("p (b m) -> p b m", b=2),
-            raw_t[0][:, 0:H].rearrange("p (b m) -> p b m", b=2),
-            first_t[:, 0:2].unsqueeze(2).to_broadcast([P, 2, P]),
-            ALU.mult,
-        )
-        fetch_raw(2, (0, 1))
-        turn_back(0, (0, 1))
-        weigh(0, (2, 3))
-        centre0 = keep.tile([P, V], F32, name="centre0", tag="raw0")
-        fetch_scaled(centre0, 0, D)
-        centre1 = keep.tile([P, V], F32, name="centre1", tag="first_t")
-        fetch_scaled(centre1, 1, D)
+        fetch_scaled(term[0], 0, 0)
+        fetch_raw(0, (0, 1, 2, 3), raw[0])
+        fetch_scaled(term[1], 0, 1)
+        fetch_raw(1, (0, 1, 2, 3), raw[1])
+        fetch_scaled(term[2], 0, 2)
+        nc.vector.tensor_tensor(partial[0][:], term[0][:], term[1][:], ALU.add)
+        fetch_raw(2, (0, 1), raw[2])
+        weigh(0, (0, 1, 2, 3))
+        fetch_scaled(centre[0], 0, D)
+        nc.vector.tensor_tensor(partial[1][:], partial[0][:], term[2][:], ALU.add)
+        fetch_scaled(centre[1], 1, D)
         weigh(1, (0, 1))
-        fetch_raw(2, (2, 3))
-        for cols in halves:
-            nc.vector.tensor_tensor(partial[1][:, cols], partial[0][:, cols], centre0[:, cols], ALU.add)
-        for cols in halves:
-            nc.vector.tensor_tensor(res[0][:, cols], partial[1][:, cols], scaled[2][:, cols], ALU.add)
+        fetch_raw(2, (2, 3), raw[1])
+        for h in range(2):
+            cols = slice(h * HALF_V, (h + 1) * HALF_V)
+            nc.vector.tensor_tensor(res[0][:, cols], partial[1][:, cols], centre[0][:, cols], ALU.add)
             nc.sync.dma_start(out[0:P, cols], res[0][:, cols])
         weigh(1, (2, 3))
         weigh(2, (0, 1))
         weigh(2, (2, 3))
-        finish(0, nc.sync)
-        finish(1, nc.sync)
+        for i, blocks in enumerate(pieces):
+            cols = slice(blocks[0] * P, (blocks[-1] + 1) * P)
+            nc.vector.tensor_tensor(res[1][:, cols], sums[i][:, 0 : len(blocks) * P], centre[1][:, cols], ALU.add)
+            nc.sync.dma_start(out[P:N, cols], res[1][:, cols])

@@ -131,10 +131,10 @@ def tile_picked_grand_none_p_kernel(tc, x_words, x_scales, w1, gate, offs, cen, 
 
         term = [keep.tile([P, V], F32, name=f"term{d}") for d in range(D)]
         partial = [keep.tile([P, V], F32, name=f"partial{i}") for i in range(2)]
-        raw = [keep.tile([P, V], F32, name=f"raw{d}") for d in range(D)]
+        raw = [keep.tile([P, HALF_V], F32, name=f"raw{i}") for i in range(3)]
         weighted = [keep.tile([P, V], F32, name=f"weighted{d}") for d in range(D)]
         res = [keep.tile([P, V], F32, name=f"res{m}") for m in range(2)]
-        turned_banks = [bank(number, f"turned{i}") for i, number in enumerate((5, 6, 7, 0))]
+        turned_banks = {}
         pieces = ((0, 1), (2,), (3,))
         sums = [bank(2 + i, f"sum{i}") for i in range(len(pieces))]
         centre = [keep.tile([P, V], F32, name=f"centre{m}") for m in range(2)]
@@ -143,13 +143,14 @@ def tile_picked_grand_none_p_kernel(tc, x_words, x_scales, w1, gate, offs, cen, 
             nc.vector.tensor_tensor(dst[:], y[m][:].indirect(lists[d][:]), factor[d][:], ALU.mult)
 
         def turned(d, b):
-            return turned_banks[d if d < D - 1 else d + b // 2][:, block(b)]
+            return turned_banks[d, b // 2][:, block(b % 2)]
 
-        def fetch_raw(d, blocks, dst):
-            lo, hi = blocks[0] * P, (blocks[-1] + 1) * P
-            nc.scalar.activation(dst[:, lo:hi], y[1][:].indirect(lists[d][:, lo // PER_COLUMN : hi // PER_COLUMN]), COPY)
-            for b in blocks:
-                nc.tensor.transpose(turned(d, b), dst[:, block(b)], ident[:])
+        def fetch_raw(d, h, dst, number):
+            entries = slice(h * HALF_V // PER_COLUMN, (h + 1) * HALF_V // PER_COLUMN)
+            nc.scalar.activation(dst[:], y[1][:].indirect(lists[d][:, entries]), COPY)
+            turned_banks[d, h] = bank(number, f"turned{d}_{h}")
+            for b in range(2):
+                nc.tensor.transpose(turned(d, 2 * h + b), dst[:, block(b)], ident[:])
 
         def weigh(d, blocks):
             for b in blocks:
@@ -167,18 +168,21 @@ def tile_picked_grand_none_p_kernel(tc, x_words, x_scales, w1, gate, offs, cen, 
                 )
 
         fetch_scaled(term[0], 0, 0)
-        fetch_raw(0, (0, 1, 2, 3), raw[0])
         fetch_scaled(term[1], 0, 1)
-        fetch_raw(1, (0, 1, 2, 3), raw[1])
         fetch_scaled(term[2], 0, 2)
         nc.vector.tensor_tensor(partial[0][:], term[0][:], term[1][:], ALU.add)
-        fetch_raw(2, (0, 1), raw[2])
-        weigh(0, (0, 1, 2, 3))
         fetch_scaled(centre[0], 0, D)
         nc.vector.tensor_tensor(partial[1][:], partial[0][:], term[2][:], ALU.add)
         fetch_scaled(centre[1], 1, D)
+        fetch_raw(0, 0, raw[0], 5)
+        fetch_raw(0, 1, raw[1], 1)
+        fetch_raw(1, 0, raw[2], 6)
+        weigh(0, (0, 1))
+        fetch_raw(1, 1, raw[0], 7)
+        weigh(0, (2, 3))
+        fetch_raw(2, 0, raw[1], 0)
         weigh(1, (0, 1))
-        fetch_raw(2, (2, 3), raw[1])
+        fetch_raw(2, 1, raw[2], 5)
         for h in range(2):
             cols = slice(h * HALF_V, (h + 1) * HALF_V)
             nc.vector.tensor_tensor(res[0][:, cols], partial[1][:, cols], centre[0][:, cols], ALU.add)

@@ -139,8 +139,9 @@ def tile_picked_grand_none_p_kernel(tc, x_words, x_scales, w1, gate, offs, cen, 
         sums = [bank(2 + i, f"sum{i}") for i in range(len(pieces))]
         centre = [keep.tile([P, V], F32, name=f"centre{m}") for m in range(2)]
 
-        def fetch_scaled(dst, m, d):
-            nc.vector.tensor_tensor(dst[:], y[m][:].indirect(lists[d][:]), factor[d][:], ALU.mult)
+        def fetch_scaled(dst, m, d, lo=0, hi=V):
+            entries = slice(lo // PER_COLUMN, hi // PER_COLUMN)
+            nc.vector.tensor_tensor(dst[:, lo:hi], y[m][:].indirect(lists[d][:, entries]), factor[d][:, lo:hi], ALU.mult)
 
         def turned(d, b):
             return turned_banks[d, b // 2][:, block(b % 2)]
@@ -167,30 +168,34 @@ def tile_picked_grand_none_p_kernel(tc, x_words, x_scales, w1, gate, offs, cen, 
                     is_transpose=True,
                 )
 
+        def finish(i):
+            blocks = pieces[i]
+            cols = slice(blocks[0] * P, (blocks[-1] + 1) * P)
+            nc.vector.tensor_tensor(res[1][:, cols], sums[i][:, 0 : len(blocks) * P], centre[1][:, cols], ALU.add)
+            nc.sync.dma_start(out[P:N, cols], res[1][:, cols])
+
         fetch_scaled(term[0], 0, 0)
         fetch_scaled(term[1], 0, 1)
         fetch_scaled(term[2], 0, 2)
         nc.vector.tensor_tensor(partial[0][:], term[0][:], term[1][:], ALU.add)
         fetch_scaled(centre[0], 0, D)
         nc.vector.tensor_tensor(partial[1][:], partial[0][:], term[2][:], ALU.add)
-        fetch_scaled(centre[1], 1, D)
+        fetch_scaled(centre[1], 1, D, 0, HALF_V)
+        nc.vector.tensor_tensor(res[0][:], partial[1][:], centre[0][:], ALU.add)
+        nc.sync.dma_start(out[0:P, :], res[0][:])
         fetch_raw(0, 0, raw[0], 5)
-        fetch_raw(0, 1, raw[1], 1)
-        fetch_raw(1, 0, raw[2], 6)
+        fetch_raw(1, 0, raw[1], 1)
+        fetch_raw(2, 0, raw[2], 6)
         weigh(0, (0, 1))
-        fetch_raw(1, 1, raw[0], 7)
-        weigh(0, (2, 3))
-        fetch_raw(2, 0, raw[1], 0)
+        fetch_raw(0, 1, raw[0], 7)
         weigh(1, (0, 1))
-        fetch_raw(2, 1, raw[2], 5)
-        for h in range(2):
-            cols = slice(h * HALF_V, (h + 1) * HALF_V)
-            nc.vector.tensor_tensor(res[0][:, cols], partial[1][:, cols], centre[0][:, cols], ALU.add)
-            nc.sync.dma_start(out[0:P, cols], res[0][:, cols])
-        weigh(1, (2, 3))
+        fetch_raw(1, 1, raw[1], 0)
         weigh(2, (0, 1))
-        weigh(2, (2, 3))
-        for i, blocks in enumerate(pieces):
-            cols = slice(blocks[0] * P, (blocks[-1] + 1) * P)
-            nc.vector.tensor_tensor(res[1][:, cols], sums[i][:, 0 : len(blocks) * P], centre[1][:, cols], ALU.add)
-            nc.sync.dma_start(out[P:N, cols], res[1][:, cols])
+        finish(0)
+        fetch_raw(2, 1, raw[2], 5)
+        for b in (2, 3):
+            fetch_scaled(centre[1], 1, D, b * P, (b + 1) * P)
+        for d in range(D):
+            weigh(d, (2, 3))
+        finish(1)
+        finish(2)

@@ -40,12 +40,12 @@ def tile_picked_grand_none_p_kernel(tc, x_words, x_scales, w1, gate, offs, cen, 
         offs_sb = keep.tile([P, S // PER_COLUMN], U16, name="offs_sb")
         lists = [keep.tile([P, V // PER_COLUMN], U16, name=f"list{d}") for d in range(D + 1)]
         words = keep.tile([P, T], U32, name="words", align_bytes=64)
-        scales = keep.tile([P, T], U8, name="scales", align_bytes=64)
+        scales = keep.tile([P, T], U8, name="scales", tag="scales_w_raw1_y0", align_bytes=64)
         plane = keep.tile([P, S], U8, name="plane", align_bytes=64)
-        w_raw = [keep.tile([P, PACK, P], F32, name=f"w_raw{m}", align_bytes=64) for m in range(2)]
+        w_raw = [keep.tile([P, PACK, P], F32, name="w_raw0", align_bytes=64)]
         gate_rows = keep.tile([P, D, P], F32, name="gate_rows")
         gate_t = keep.tile([P, D, BLOCKS], F32, name="gate_t")
-        centre_t = keep.tile([P, BLOCKS], F32, name="centre_t", tag="centre_t_then_w_bf1", align_bytes=64)
+        centre_t = keep.tile([P, BLOCKS], F32, name="centre_t", tag="centre_then_w_bf1", align_bytes=64)
         ident = keep.tile([P, P], F32, name="ident")
 
         first_scale_row = P - SCALE_ROWS
@@ -61,7 +61,6 @@ def tile_picked_grand_none_p_kernel(tc, x_words, x_scales, w1, gate, offs, cen, 
         nc.sync.dma_start(lists[0][:], pos1)
         nc.sync.dma_start(lists[1][:], pos2)
         nc.sync.dma_start(words[:].bitcast(I32), x_words[0].rearrange("p n t -> p (n t)").bitcast(I32))
-        nc.sync.dma_start(w_raw[1][:], w_rows[:, :, P:N])
         nc.sync.dma_start(lists[2][:], pos3)
         nc.sync.dma_start(lists[D][:], cen)
 
@@ -88,6 +87,8 @@ def tile_picked_grand_none_p_kernel(tc, x_words, x_scales, w1, gate, offs, cen, 
         nc.vector.tensor_copy(picked_scales[:], scales[:].indirect(offs_sb[:]))
         for i in range(4):
             nc.sync.dma_start(plane[i:P:32, :].bitcast(I32), picked_scales[first_scale_row + i : P : 4, :].bitcast(I32))
+        w_raw.append(keep.tile([P, PACK, P], F32, name="w_raw1", tag="scales_w_raw1_y0", align_bytes=64))
+        nc.sync.dma_start(w_raw[1][:], w_rows[:, :, P:N])
 
         quantize_w(0, w_bf0)
 
@@ -99,10 +100,13 @@ def tile_picked_grand_none_p_kernel(tc, x_words, x_scales, w1, gate, offs, cen, 
                 nc.tensor.transpose(spread[:, block(b)], columns[:, b : b + 1].to_broadcast([P, P]), ident[:])
             nc.scalar.copy(factor[d][:], spread[:])
 
-        w_bf1 = keep.tile([P, P, PACK], BF16, name="w_bf1", tag="centre_t_then_w_bf1", align_bytes=64)
+        w_bf1 = keep.tile([P, P, PACK], BF16, name="w_bf1", tag="centre_then_w_bf1", align_bytes=64)
 
         picked = [keep.tile([P, HALF_S], U32, name=f"picked{h}", align_bytes=64) for h in range(2)]
-        y = [keep.tile([P, S], F32, name=f"y{m}") for m in range(2)]
+        y = [
+            keep.tile([P, S], F32, name="y0", tag="scales_w_raw1_y0", align_bytes=64),
+            keep.tile([P, S], F32, name="y1"),
+        ]
 
         def project(m, number, lo, hi, copy_out):
             h = lo // HALF_S
@@ -122,6 +126,17 @@ def tile_picked_grand_none_p_kernel(tc, x_words, x_scales, w1, gate, offs, cen, 
             entries = slice(h * HALF_S // PER_COLUMN, (h + 1) * HALF_S // PER_COLUMN)
             nc.vector.tensor_copy(picked[h][:], words[:].indirect(offs_sb[:, entries]))
         quantize_w(1, w_bf1)
+        warm = bank(6, "warm")
+        for b in range(4):
+            nc.tensor.matmul_mx(
+                out=warm[:, block(b)],
+                lhsT=w_codes[0][:].bitcast(FP8X4),
+                lhsT_scale=w_scales[0][:],
+                rhs=w_codes[0][:].bitcast(FP8X4),
+                rhs_scale=plane[:, 0:P],
+                start=True,
+                stop=True,
+            )
         three_quarters = HALF_S + HALF_S // 2
         project(0, 0, 0, HALF_S, nc.scalar.copy)
         project(0, 2, HALF_S, three_quarters, nc.vector.tensor_copy)

@@ -11,6 +11,7 @@ SCALE_ROWS = K // 32
 PER_COLUMN = 16
 HALF_S = S // 2
 HALF_V = V // 2
+LAST = BLOCKS - 1
 FLOPS = 2 * K * N * S
 
 F32 = mybir.dt.float32
@@ -152,11 +153,13 @@ def tile_picked_grand_none_p_kernel(tc, x_words, x_scales, w1, gate, offs, cen, 
         turned_banks = {}
         pieces = ((0, 1), (2,), (3,))
         sums = [bank(2 + i, f"sum{i}") for i in range(len(pieces))]
-        centre = [keep.tile([P, V], F32, name=f"centre{m}") for m in range(2)]
+        centre0 = keep.tile([P, V], F32, name="centre0")
+        centre_ends = keep.tile([P, 3 * P], F32, name="centre_ends")
+        centre1 = [centre_ends[:, 0:HALF_V], weighted[D - 1][:, block(1)], centre_ends[:, block(2)]]
 
         def fetch_scaled(dst, m, d, lo=0, hi=V):
             entries = slice(lo // PER_COLUMN, hi // PER_COLUMN)
-            nc.vector.tensor_tensor(dst[:, lo:hi], y[m][:].indirect(lists[d][:, entries]), factor[d][:, lo:hi], ALU.mult)
+            nc.vector.tensor_tensor(dst, y[m][:].indirect(lists[d][:, entries]), factor[d][:, lo:hi], ALU.mult)
 
         def turned(d, b):
             return turned_banks[d, b // 2][:, block(b % 2)]
@@ -186,17 +189,17 @@ def tile_picked_grand_none_p_kernel(tc, x_words, x_scales, w1, gate, offs, cen, 
         def finish(i):
             blocks = pieces[i]
             cols = slice(blocks[0] * P, (blocks[-1] + 1) * P)
-            nc.vector.tensor_tensor(res[1][:, cols], sums[i][:, 0 : len(blocks) * P], centre[1][:, cols], ALU.add)
+            nc.vector.tensor_tensor(res[1][:, cols], sums[i][:, 0 : len(blocks) * P], centre1[i], ALU.add)
             nc.sync.dma_start(out[P:N, cols], res[1][:, cols])
 
-        fetch_scaled(term[0], 0, 0)
-        fetch_scaled(term[1], 0, 1)
-        fetch_scaled(term[2], 0, 2)
+        fetch_scaled(term[0][:], 0, 0)
+        fetch_scaled(term[1][:], 0, 1)
+        fetch_scaled(term[2][:], 0, 2)
         nc.vector.tensor_tensor(partial[0][:], term[0][:], term[1][:], ALU.add)
-        fetch_scaled(centre[0], 0, D)
+        fetch_scaled(centre0[:], 0, D)
         nc.vector.tensor_tensor(partial[1][:], partial[0][:], term[2][:], ALU.add)
-        fetch_scaled(centre[1], 1, D, 0, HALF_V)
-        nc.vector.tensor_tensor(res[0][:], partial[1][:], centre[0][:], ALU.add)
+        fetch_scaled(centre1[0], 1, D, 0, HALF_V)
+        nc.vector.tensor_tensor(res[0][:], partial[1][:], centre0[:], ALU.add)
         nc.sync.dma_start(out[0:P, :], res[0][:])
         fetch_raw(0, 0, raw[0], 5)
         fetch_raw(1, 0, raw[1], 1)
@@ -208,9 +211,12 @@ def tile_picked_grand_none_p_kernel(tc, x_words, x_scales, w1, gate, offs, cen, 
         weigh(2, (0, 1))
         finish(0)
         fetch_raw(2, 1, raw[2], 5)
-        for b in (2, 3):
-            fetch_scaled(centre[1], 1, D, b * P, (b + 1) * P)
-        for d in range(D):
-            weigh(d, (2, 3))
+        fetch_scaled(centre1[1], 1, D, HALF_V, LAST * P)
+        weigh(0, (2, 3))
+        weigh(1, (2, 3))
+        centre_raw = raw[1][:, 0:P]
+        nc.scalar.activation(centre_raw, y[1][:].indirect(lists[D][:, LAST * P // PER_COLUMN :]), COPY)
+        nc.vector.tensor_tensor(centre1[2], centre_raw, factor[D][:, block(LAST)], ALU.mult)
+        weigh(2, (2, 3))
         finish(1)
         finish(2)

@@ -103,7 +103,7 @@ def tile_picked_grand_none_p_kernel(tc, x_words, x_scales, w1, gate, offs, cen, 
 
         w_bf1 = keep.tile([P, P, PACK], BF16, name="w_bf1", tag="centre_then_w_bf1", align_bytes=64)
 
-        picked = [keep.tile([P, HALF_S], U32, name=f"picked{h}", align_bytes=64) for h in range(2)]
+        picked = [keep.tile([P, HALF_S], U32, name=f"picked{h}", tag=f"picked{h}", align_bytes=64) for h in range(2)]
         y = [
             keep.tile([P, S], F32, name="y0", tag="scales_w_raw1_y0", align_bytes=64),
             keep.tile([P, S], F32, name="y1"),
@@ -141,9 +141,11 @@ def tile_picked_grand_none_p_kernel(tc, x_words, x_scales, w1, gate, offs, cen, 
         three_quarters = HALF_S + HALF_S // 2
         project(0, 0, 0, HALF_S, nc.scalar.copy)
         project(0, 2, HALF_S, three_quarters, nc.vector.tensor_copy)
-        project(0, 3, three_quarters, S, nc.scalar.copy)
-        project(1, 1, 0, HALF_S, nc.scalar.copy)
-        project(1, 4, HALF_S, S, nc.scalar.copy)
+        project(0, 3, three_quarters, S - P, nc.scalar.copy)
+        project(0, 5, S - P, S, nc.scalar.copy)
+        quarter = S // 4
+        for i, number in enumerate((1, 4, 7, 0)):
+            project(1, number, i * quarter, (i + 1) * quarter, nc.scalar.copy)
 
         term = [keep.tile([P, V], F32, name=f"term{d}") for d in range(D)]
         partial = [keep.tile([P, V], F32, name=f"partial{i}") for i in range(2)]
@@ -192,11 +194,14 @@ def tile_picked_grand_none_p_kernel(tc, x_words, x_scales, w1, gate, offs, cen, 
             nc.vector.tensor_tensor(res[1][:, cols], sums[i][:, 0 : len(blocks) * P], centre1[i], ALU.add)
             nc.sync.dma_start(out[P:N, cols], res[1][:, cols])
 
+        centre_raw0 = keep.tile([P, P], F32, name="centre_raw0", tag="picked1", align_bytes=64)
+        nc.scalar.activation(centre_raw0[:], y[0][:].indirect(lists[D][:, LAST * P // PER_COLUMN :]), COPY)
         fetch_scaled(term[0][:], 0, 0)
         fetch_scaled(term[1][:], 0, 1)
         fetch_scaled(term[2][:], 0, 2)
         nc.vector.tensor_tensor(partial[0][:], term[0][:], term[1][:], ALU.add)
-        fetch_scaled(centre0[:], 0, D)
+        fetch_scaled(centre0[:, 0 : LAST * P], 0, D, 0, LAST * P)
+        nc.vector.tensor_tensor(centre0[:, block(LAST)], centre_raw0[:], factor[D][:, block(LAST)], ALU.mult)
         nc.vector.tensor_tensor(partial[1][:], partial[0][:], term[2][:], ALU.add)
         fetch_scaled(centre1[0], 1, D, 0, HALF_V)
         nc.vector.tensor_tensor(res[0][:], partial[1][:], centre0[:], ALU.add)

@@ -12,6 +12,7 @@ PER_COLUMN = 16
 HALF_S = S // 2
 HALF_V = V // 2
 LAST = BLOCKS - 1
+FUSED1 = 320
 FLOPS = 2 * K * N * S
 
 F32 = mybir.dt.float32
@@ -155,9 +156,7 @@ def tile_picked_grand_none_p_kernel(tc, x_words, x_scales, w1, gate, offs, cen, 
         turned_banks = {}
         pieces = ((0, 1), (2,), (3,))
         sums = [bank(2 + i, f"sum{i}") for i in range(len(pieces))]
-        centre0 = keep.tile([P, V], F32, name="centre0")
-        centre_ends = keep.tile([P, 3 * P], F32, name="centre_ends")
-        centre1 = [centre_ends[:, 0:HALF_V], weighted[D - 1][:, block(1)], centre_ends[:, block(2)]]
+        centre = [keep.tile([P, V], F32, name=f"centre{m}") for m in range(2)]
 
         def fetch_scaled(dst, m, d, lo=0, hi=V):
             entries = slice(lo // PER_COLUMN, hi // PER_COLUMN)
@@ -191,7 +190,7 @@ def tile_picked_grand_none_p_kernel(tc, x_words, x_scales, w1, gate, offs, cen, 
         def finish(i):
             blocks = pieces[i]
             cols = slice(blocks[0] * P, (blocks[-1] + 1) * P)
-            nc.vector.tensor_tensor(res[1][:, cols], sums[i][:, 0 : len(blocks) * P], centre1[i], ALU.add)
+            nc.vector.tensor_tensor(res[1][:, cols], sums[i][:, 0 : len(blocks) * P], centre[1][:, cols], ALU.add)
             nc.sync.dma_start(out[P:N, cols], res[1][:, cols])
 
         centre_raw0 = keep.tile([P, P], F32, name="centre_raw0", tag="picked1", align_bytes=64)
@@ -200,11 +199,11 @@ def tile_picked_grand_none_p_kernel(tc, x_words, x_scales, w1, gate, offs, cen, 
         fetch_scaled(term[1][:], 0, 1)
         fetch_scaled(term[2][:], 0, 2)
         nc.vector.tensor_tensor(partial[0][:], term[0][:], term[1][:], ALU.add)
-        fetch_scaled(centre0[:, 0 : LAST * P], 0, D, 0, LAST * P)
-        nc.vector.tensor_tensor(centre0[:, block(LAST)], centre_raw0[:], factor[D][:, block(LAST)], ALU.mult)
+        fetch_scaled(centre[0][:, 0 : LAST * P], 0, D, 0, LAST * P)
+        nc.vector.tensor_tensor(centre[0][:, block(LAST)], centre_raw0[:], factor[D][:, block(LAST)], ALU.mult)
         nc.vector.tensor_tensor(partial[1][:], partial[0][:], term[2][:], ALU.add)
-        fetch_scaled(centre1[0], 1, D, 0, HALF_V)
-        nc.vector.tensor_tensor(res[0][:], partial[1][:], centre0[:], ALU.add)
+        fetch_scaled(centre[1][:, 0:FUSED1], 1, D, 0, FUSED1)
+        nc.vector.tensor_tensor(res[0][:], partial[1][:], centre[0][:], ALU.add)
         nc.sync.dma_start(out[0:P, :], res[0][:])
         fetch_raw(0, 0, raw[0], 5)
         fetch_raw(1, 0, raw[1], 1)
@@ -216,12 +215,11 @@ def tile_picked_grand_none_p_kernel(tc, x_words, x_scales, w1, gate, offs, cen, 
         weigh(2, (0, 1))
         finish(0)
         fetch_raw(2, 1, raw[2], 5)
-        fetch_scaled(centre1[1], 1, D, HALF_V, LAST * P)
         weigh(0, (2, 3))
         weigh(1, (2, 3))
-        centre_raw = raw[1][:, 0:P]
-        nc.scalar.activation(centre_raw, y[1][:].indirect(lists[D][:, LAST * P // PER_COLUMN :]), COPY)
-        nc.vector.tensor_tensor(centre1[2], centre_raw, factor[D][:, block(LAST)], ALU.mult)
+        nc.scalar.activation(raw[1][:, 0 : V - FUSED1], y[1][:].indirect(lists[D][:, FUSED1 // PER_COLUMN :]), COPY)
+        for lo, hi in ((FUSED1, LAST * P), (LAST * P, V)):
+            nc.vector.tensor_tensor(centre[1][:, lo:hi], raw[1][:, lo - FUSED1 : hi - FUSED1], factor[D][:, lo:hi], ALU.mult)
         weigh(2, (2, 3))
         finish(1)
         finish(2)

@@ -9,10 +9,12 @@ PACK = 4
 BLOCKS = V // P
 SCALE_ROWS = K // 32
 PER_COLUMN = 16
-HALF_S = S // 2
+QUARTERS = 4
+Q = S // QUARTERS
 HALF_V = V // 2
 LAST = BLOCKS - 1
-FUSED1 = 320
+OWN = LAST * P
+SHARED = 2
 FLOPS = 2 * K * N * S
 
 F32 = mybir.dt.float32
@@ -30,10 +32,15 @@ def block(b):
     return slice(b * P, (b + 1) * P)
 
 
+def entries(lo, hi):
+    return slice(lo // PER_COLUMN, hi // PER_COLUMN)
+
+
 def tile_picked_grand_none_p_kernel(tc, x_words, x_scales, w1, gate, offs, cen, pos1, pos2, pos3, out):
     nc = tc.nc
     with ExitStack() as ctx:
         keep = ctx.enter_context(tc.tile_pool(name="keep", bufs=1))
+        turns = ctx.enter_context(tc.tile_pool(name="turns", bufs=1))
         psum = ctx.enter_context(tc.psum_pool(name="psum", bufs=1))
 
         def bank(number, name):
@@ -42,7 +49,7 @@ def tile_picked_grand_none_p_kernel(tc, x_words, x_scales, w1, gate, offs, cen, 
         offs_sb = keep.tile([P, S // PER_COLUMN], U16, name="offs_sb")
         lists = [keep.tile([P, V // PER_COLUMN], U16, name=f"list{d}") for d in range(D + 1)]
         words = keep.tile([P, T], U32, name="words", align_bytes=64)
-        scales = keep.tile([P, T], U8, name="scales", tag="scales_w_raw1_y0", align_bytes=64)
+        scales = keep.tile([P, T], U8, name="scales", align_bytes=64)
         plane = keep.tile([P, S], U8, name="plane", align_bytes=64)
         w_raw = [keep.tile([P, PACK, P], F32, name="w_raw0", align_bytes=64)]
         gate_rows = keep.tile([P, D, P], F32, name="gate_rows")
@@ -56,13 +63,15 @@ def tile_picked_grand_none_p_kernel(tc, x_words, x_scales, w1, gate, offs, cen, 
         nc.vector.memset(gate_rows[0:first_gate_row, :, :], 0.0)
         nc.vector.memset(plane[:].bitcast(I32), 0)
         nc.sync.dma_start(offs_sb[:], offs)
-        nc.scalar.dma_start(scales[first_scale_row:P, :].bitcast(I32), x_scales[0].bitcast(I32))
+        nc.sync.dma_start(scales[first_scale_row:P, :].bitcast(I32), x_scales[0].bitcast(I32))
         nc.scalar.dma_start(gate_rows[first_gate_row:P, :, :], gate[:, 0, :].rearrange("d (b v) -> b d v", b=BLOCKS))
         w_rows = w1.rearrange("(p j) n -> p j n", j=PACK)
         nc.sync.dma_start(w_raw[0][:], w_rows[:, :, 0:P])
         nc.sync.dma_start(lists[0][:], pos1)
         nc.sync.dma_start(lists[1][:], pos2)
         nc.sync.dma_start(words[:].bitcast(I32), x_words[0].rearrange("p n t -> p (n t)").bitcast(I32))
+        w_raw.append(turns.tile([P, PACK, P], F32, name="w_raw1", offset=T - 2 * Q, align_bytes=64))
+        nc.sync.dma_start(w_raw[1][:], w_rows[:, :, P:N])
         nc.sync.dma_start(lists[2][:], pos3)
         nc.sync.dma_start(lists[D][:], cen)
 
@@ -89,137 +98,124 @@ def tile_picked_grand_none_p_kernel(tc, x_words, x_scales, w1, gate, offs, cen, 
         nc.vector.tensor_copy(picked_scales[:], scales[:].indirect(offs_sb[:]))
         for i in range(4):
             nc.sync.dma_start(plane[i:P:32, :].bitcast(I32), picked_scales[first_scale_row + i : P : 4, :].bitcast(I32))
-        w_raw.append(keep.tile([P, PACK, P], F32, name="w_raw1", tag="scales_w_raw1_y0", align_bytes=64))
-        nc.sync.dma_start(w_raw[1][:], w_rows[:, :, P:N])
 
         quantize_w(0, w_bf0)
 
-        factor = [keep.tile([P, V], F32, name=f"factor{d}") for d in range(D + 1)]
+        factor = [keep.tile([P, OWN if d < SHARED else V], F32, name=f"factor{d}") for d in range(D + 1)]
         for d in range(D + 1):
             spread = bank(d, f"spread{d}")
             columns = gate_t[:, d, :] if d < D else centre_t[:]
-            for b in range(BLOCKS):
+            count = LAST if d < SHARED else BLOCKS
+            for b in range(count):
                 nc.tensor.transpose(spread[:, block(b)], columns[:, b : b + 1].to_broadcast([P, P]), ident[:])
-            nc.scalar.copy(factor[d][:], spread[:])
+            nc.scalar.copy(factor[d][:], spread[:, 0 : count * P])
 
         w_bf1 = keep.tile([P, P, PACK], BF16, name="w_bf1", tag="centre_then_w_bf1", align_bytes=64)
 
-        picked = [keep.tile([P, HALF_S], U32, name=f"picked{h}", tag=f"picked{h}", align_bytes=64) for h in range(2)]
         y = [
-            keep.tile([P, S], F32, name="y0", tag="scales_w_raw1_y0", align_bytes=64),
+            turns.tile([P, S], F32, name="y0", offset=0, align_bytes=64),
             keep.tile([P, S], F32, name="y1"),
         ]
+        picked = []
+
+        def pick(q, tile):
+            picked.append(tile)
+            nc.vector.tensor_copy(picked[q][:], words[:].indirect(offs_sb[:, entries(q * Q, (q + 1) * Q)]))
 
         def project(m, number, lo, hi, copy_out):
-            h = lo // HALF_S
+            q = lo // Q
             acc = bank(number, f"acc{m}_{lo}")
             nc.tensor.matmul_mx(
                 out=acc[:, 0 : hi - lo],
                 lhsT=w_codes[m][:].bitcast(FP8X4),
                 lhsT_scale=w_scales[m][:],
-                rhs=picked[h][:, lo - h * HALF_S : hi - h * HALF_S].bitcast(FP8X4),
+                rhs=picked[q][:, lo - q * Q : hi - q * Q].bitcast(FP8X4),
                 rhs_scale=plane[:, lo:hi],
                 start=True,
                 stop=True,
             )
             copy_out(y[m][:, lo:hi], acc[:, 0 : hi - lo])
 
-        for h in range(2):
-            entries = slice(h * HALF_S // PER_COLUMN, (h + 1) * HALF_S // PER_COLUMN)
-            nc.vector.tensor_copy(picked[h][:], words[:].indirect(offs_sb[:, entries]))
+        for q in range(2):
+            pick(q, keep.tile([P, Q], U32, name=f"picked{q}", align_bytes=64))
         quantize_w(1, w_bf1)
-        warm = bank(6, "warm")
-        for b in range(4):
-            nc.tensor.matmul_mx(
-                out=warm[:, block(b)],
-                lhsT=w_codes[0][:].bitcast(FP8X4),
-                lhsT_scale=w_scales[0][:],
-                rhs=w_codes[0][:].bitcast(FP8X4),
-                rhs_scale=plane[:, 0:P],
-                start=True,
-                stop=True,
-            )
-        three_quarters = HALF_S + HALF_S // 2
-        project(0, 0, 0, HALF_S, nc.scalar.copy)
-        project(0, 2, HALF_S, three_quarters, nc.vector.tensor_copy)
-        project(0, 3, three_quarters, S - P, nc.scalar.copy)
-        project(0, 5, S - P, S, nc.scalar.copy)
-        quarter = S // 4
-        for i, number in enumerate((1, 4, 7, 0)):
-            project(1, number, i * quarter, (i + 1) * quarter, nc.scalar.copy)
+        for q in range(2, 4):
+            pick(q, turns.tile([P, Q], U32, name=f"picked{q}", offset=T + 4 * Q * (q - 2), align_bytes=64))
+        project(0, 0, 0, Q, nc.scalar.copy)
+        project(0, 1, Q, 2 * Q, nc.scalar.copy)
+        project(1, 2, 0, Q, nc.scalar.copy)
+        project(1, 3, Q, 2 * Q, nc.scalar.copy)
+        project(0, 4, 2 * Q, 3 * Q, nc.vector.tensor_copy)
+        project(1, 5, 2 * Q, 3 * Q, nc.scalar.copy)
+        project(0, 6, 3 * Q, S - P, nc.vector.tensor_copy)
+        project(0, 7, S - P, S, nc.scalar.copy)
+        project(1, 0, 3 * Q, S - P, nc.vector.tensor_copy)
+        project(1, 1, S - P, S, nc.scalar.copy)
 
-        term = [keep.tile([P, V], F32, name=f"term{d}") for d in range(D)]
-        partial = [keep.tile([P, V], F32, name=f"partial{i}") for i in range(2)]
-        raw = [keep.tile([P, HALF_V], F32, name=f"raw{i}") for i in range(3)]
-        weighted = [keep.tile([P, V], F32, name=f"weighted{d}") for d in range(D)]
-        res = [keep.tile([P, V], F32, name=f"res{m}") for m in range(2)]
-        turned_banks = {}
-        pieces = ((0, 1), (2,), (3,))
-        sums = [bank(2 + i, f"sum{i}") for i in range(len(pieces))]
+        raw0 = [keep.tile([P, P], F32, name=f"raw0_{d}") for d in range(SHARED)]
+        raw1 = [keep.tile([P, HALF_V], F32, name=f"raw1_{d}") for d in range(D)]
+        weighted = [[keep.tile([P, 3 * P], F32, name=f"weighted{r}_{d}") for d in range(D)] for r in range(2)]
+        term = [keep.tile([P, OWN if d < SHARED else V], F32, name=f"term{d}") for d in range(D)]
+        partial = [keep.tile([P, OWN], F32, name="partial0"), keep.tile([P, V], F32, name="partial1")]
         centre = [keep.tile([P, V], F32, name=f"centre{m}") for m in range(2)]
+        res = [keep.tile([P, V], F32, name=f"res{m}") for m in range(2)]
+        turned = {}
 
-        def fetch_scaled(dst, m, d, lo=0, hi=V):
-            entries = slice(lo // PER_COLUMN, hi // PER_COLUMN)
-            nc.vector.tensor_tensor(dst, y[m][:].indirect(lists[d][:, entries]), factor[d][:, lo:hi], ALU.mult)
+        def fetch_scaled(dst, m, d, hi):
+            nc.vector.tensor_tensor(dst, y[m][:].indirect(lists[d][:, entries(0, hi)]), factor[d][:, 0:hi], ALU.mult)
 
-        def turned(d, b):
-            return turned_banks[d, b // 2][:, block(b % 2)]
-
-        def fetch_raw(d, h, dst, number):
-            entries = slice(h * HALF_V // PER_COLUMN, (h + 1) * HALF_V // PER_COLUMN)
-            nc.scalar.activation(dst[:], y[1][:].indirect(lists[d][:, entries]), COPY)
-            turned_banks[d, h] = bank(number, f"turned{d}_{h}")
+        def fetch_raw(r, d, number):
+            lo = HALF_V if r == 0 else 0
+            nc.scalar.activation(raw1[d][:], y[1][:].indirect(lists[d][:, entries(lo, lo + HALF_V)]), COPY)
+            turned[r, d] = bank(number, f"turned{r}_{d}")
+            if r == 0 and d < SHARED:
+                nc.tensor.transpose(turned[r, d][:, block(2)], raw0[d][:], ident[:])
             for b in range(2):
-                nc.tensor.transpose(turned(d, 2 * h + b), dst[:, block(b)], ident[:])
+                nc.tensor.transpose(turned[r, d][:, block(b)], raw1[d][:, block(b)], ident[:])
 
-        def weigh(d, blocks):
-            for b in blocks:
-                nc.scalar.activation(weighted[d][:, block(b)], turned(d, b), COPY, scale=gate_t[:, d, b : b + 1])
-            for b in blocks:
-                i = max(b - 1, 0)
-                first, last = pieces[i][0], pieces[i][-1]
-                nc.tensor.matmul(
-                    sums[i][:, block(b - first)],
-                    weighted[d][:, block(b)],
-                    ident[:],
-                    start=(d == 0 and b == first),
-                    stop=(d == D - 1 and b == last),
-                    is_transpose=True,
-                )
+        def weigh(r, d, lo, hi, b):
+            nc.scalar.activation(weighted[r][d][:, lo:hi], turned[r, d][:, lo:hi], COPY, scale=gate_t[:, d, b : b + 1])
 
-        def finish(i):
-            blocks = pieces[i]
-            cols = slice(blocks[0] * P, (blocks[-1] + 1) * P)
-            nc.vector.tensor_tensor(res[1][:, cols], sums[i][:, 0 : len(blocks) * P], centre[1][:, cols], ALU.add)
-            nc.sync.dma_start(out[P:N, cols], res[1][:, cols])
+        def turn_back(dst, src, start, stop):
+            nc.tensor.matmul(dst, src, ident[:], start=start, stop=stop, is_transpose=True)
 
-        centre_raw0 = keep.tile([P, P], F32, name="centre_raw0", tag="picked1", align_bytes=64)
-        nc.scalar.activation(centre_raw0[:], y[0][:].indirect(lists[D][:, LAST * P // PER_COLUMN :]), COPY)
-        fetch_scaled(term[0][:], 0, 0)
-        fetch_scaled(term[1][:], 0, 1)
-        fetch_scaled(term[2][:], 0, 2)
-        nc.vector.tensor_tensor(partial[0][:], term[0][:], term[1][:], ALU.add)
-        fetch_scaled(centre[0][:, 0 : LAST * P], 0, D, 0, LAST * P)
-        nc.vector.tensor_tensor(centre[0][:, block(LAST)], centre_raw0[:], factor[D][:, block(LAST)], ALU.mult)
-        nc.vector.tensor_tensor(partial[1][:], partial[0][:], term[2][:], ALU.add)
-        fetch_scaled(centre[1][:, 0:FUSED1], 1, D, 0, FUSED1)
-        nc.vector.tensor_tensor(res[0][:], partial[1][:], centre[0][:], ALU.add)
-        nc.sync.dma_start(out[0:P, :], res[0][:])
-        fetch_raw(0, 0, raw[0], 5)
-        fetch_raw(1, 0, raw[1], 1)
-        fetch_raw(2, 0, raw[2], 6)
-        weigh(0, (0, 1))
-        fetch_raw(0, 1, raw[0], 7)
-        weigh(1, (0, 1))
-        fetch_raw(1, 1, raw[1], 0)
-        weigh(2, (0, 1))
-        finish(0)
-        fetch_raw(2, 1, raw[2], 5)
-        weigh(0, (2, 3))
-        weigh(1, (2, 3))
-        nc.scalar.activation(raw[1][:, 0 : V - FUSED1], y[1][:].indirect(lists[D][:, FUSED1 // PER_COLUMN :]), COPY)
-        for lo, hi in ((FUSED1, LAST * P), (LAST * P, V)):
-            nc.vector.tensor_tensor(centre[1][:, lo:hi], raw[1][:, lo - FUSED1 : hi - FUSED1], factor[D][:, lo:hi], ALU.mult)
-        weigh(2, (2, 3))
-        finish(1)
-        finish(2)
+        sum0 = bank(7, "sum0")
+        sum1 = [bank(b, f"sum1_{b}") for b in range(2)]
+
+        def weigh0(d):
+            count = 3 if d < SHARED else 2
+            weigh(0, d, 0, P, 2)
+            weigh(0, d, P, count * P, LAST)
+            for i in range(count):
+                turn_back(sum0[:, block(i)], weighted[0][d][:, block(i)], d == 0 and i == 0, d == D - 1 and i == count - 1)
+
+        def weigh1(d):
+            for b in range(2):
+                weigh(1, d, b * P, (b + 1) * P, b)
+                turn_back(sum1[b][:, 0:P], weighted[1][d][:, block(b)], d == 0, d == D - 1)
+
+        for d in range(SHARED):
+            nc.scalar.activation(raw0[d][:], y[0][:].indirect(lists[d][:, entries(OWN, V)]), COPY)
+        fetch_scaled(term[2][:], 0, 2, V)
+        fetch_scaled(centre[0][:], 0, D, V)
+        fetch_scaled(term[0][:], 0, 0, OWN)
+        nc.vector.tensor_tensor(partial[1][:], term[2][:], centre[0][:], ALU.add)
+        fetch_scaled(term[1][:], 0, 1, OWN)
+        nc.vector.tensor_tensor(partial[0][:], partial[1][:, 0:OWN], term[0][:], ALU.add)
+        fetch_scaled(centre[1][:], 1, D, V)
+        nc.vector.tensor_tensor(res[0][:, 0:OWN], partial[0][:], term[1][:], ALU.add)
+        nc.sync.dma_start(out[0:P, 0:OWN], res[0][:, 0:OWN])
+        for d in range(D):
+            fetch_raw(0, d, 2 + d)
+        for d in range(D):
+            weigh0(d)
+            fetch_raw(1, d, (5, 6, 2)[d])
+        nc.vector.tensor_tensor(res[1][:, HALF_V:V], sum0[:, 0:HALF_V], centre[1][:, HALF_V:V], ALU.add)
+        nc.sync.dma_start(out[P:N, HALF_V:V], res[1][:, HALF_V:V])
+        nc.vector.tensor_tensor(res[0][:, OWN:V], sum0[:, block(2)], partial[1][:, OWN:V], ALU.add)
+        nc.sync.dma_start(out[0:P, OWN:V], res[0][:, OWN:V])
+        for d in range(D):
+            weigh1(d)
+        for b in range(2):
+            nc.vector.tensor_tensor(res[1][:, block(b)], sum1[b][:, 0:P], centre[1][:, block(b)], ALU.add)
+            nc.sync.dma_start(out[P:N, block(b)], res[1][:, block(b)])

@@ -79,17 +79,16 @@ def tile_picked_grand_none_p_kernel(tc, x_words, x_scales, w1, gate, offs, cen, 
         gate_turned = bank(7, "gate_turned")
         for d in range(D):
             nc.tensor.transpose(gate_turned[:, block(d)], gate_rows[:, d, :], ident[:])
+        for d in range(D):
+            nc.tensor.matmul(gate_turned[:, block(D)], gate_rows[:, d, :], ident[:], start=d == 0, stop=d == D - 1, is_transpose=True)
         nc.scalar.activation(gate_t[:], gate_turned[:].rearrange("p (d r) -> p d r", r=P)[:, 0:D, first_gate_row:P], COPY)
-        gate_sum = keep.tile([P, 2, BLOCKS], F32, name="gate_sum")
-        nc.gpsimd.tensor_tensor(gate_sum[:, 0, :], gate_t[:, 0, :], gate_t[:, 1, :], ALU.add)
-        nc.gpsimd.tensor_tensor(gate_sum[:, 1, :], gate_sum[:, 0, :], gate_t[:, 2, :], ALU.add)
-        nc.gpsimd.tensor_scalar(centre_t[:], gate_sum[:, 1, :], -1.0, 1.0, ALU.mult, ALU.add)
+        nc.scalar.activation(centre_t[:], gate_turned[:, D * P + first_gate_row : (D + 1) * P], COPY, scale=-1.0, bias=1.0)
 
         w_codes = [keep.tile([P, P], U32, name=f"w_codes{m}", align_bytes=64) for m in range(2)]
         w_scales = [keep.tile([P, P], U8, name=f"w_scales{m}", align_bytes=64) for m in range(2)]
 
         def quantize_w(m, w_bf):
-            nc.scalar.copy(w_bf[:], w_raw[m][:].rearrange("p j n -> p n j"))
+            nc.scalar.copy(w_bf[:].rearrange("p (c i) j -> p c j i", i=4), w_raw[m][:].rearrange("p j (c i) -> p c j i", i=4))
             nc.vector.quantize_mx(out=w_codes[m][:].bitcast(FP8X4), scales=w_scales[m][:], in_=w_bf[:].rearrange("p n j -> p (n j)"))
 
         w_bf0 = keep.tile([P, P, PACK], BF16, name="w_bf0", align_bytes=64)

@@ -63,7 +63,7 @@ def tile_picked_grand_none_p_kernel(tc, x_words, x_scales, w1, gate, offs, cen, 
         nc.vector.memset(gate_rows[0:first_gate_row, :, :], 0.0)
         nc.vector.memset(plane[:].bitcast(I32), 0)
         nc.sync.dma_start(offs_sb[:], offs)
-        nc.sync.dma_start(scales[first_scale_row:P, :].bitcast(I32), x_scales[0].bitcast(I32))
+        nc.scalar.dma_start(scales[first_scale_row:P, :].bitcast(I32), x_scales[0].bitcast(I32))
         nc.scalar.dma_start(gate_rows[first_gate_row:P, :, :], gate[:, 0, :].rearrange("d (b v) -> b d v", b=BLOCKS))
         w_rows = w1.rearrange("(p j) n -> p j n", j=PACK)
         nc.sync.dma_start(w_raw[0][:], w_rows[:, :, 0:P])
@@ -156,12 +156,12 @@ def tile_picked_grand_none_p_kernel(tc, x_words, x_scales, w1, gate, offs, cen, 
         weighted = [[keep.tile([P, 3 * P], F32, name=f"weighted{r}_{d}") for d in range(D)] for r in range(2)]
         term = [keep.tile([P, OWN if d < SHARED else V], F32, name=f"term{d}") for d in range(D)]
         partial = [keep.tile([P, OWN], F32, name="partial0"), keep.tile([P, V], F32, name="partial1")]
-        centre = [keep.tile([P, V], F32, name=f"centre{m}") for m in range(2)]
+        centre0 = keep.tile([P, V], F32, name="centre0")
         res = [keep.tile([P, V], F32, name=f"res{m}") for m in range(2)]
         turned = {}
 
-        def fetch_scaled(dst, m, d, hi):
-            nc.vector.tensor_tensor(dst, y[m][:].indirect(lists[d][:, entries(0, hi)]), factor[d][:, 0:hi], ALU.mult)
+        def fetch_scaled(dst, m, d, hi, lo=0):
+            nc.vector.tensor_tensor(dst, y[m][:].indirect(lists[d][:, entries(lo, hi)]), factor[d][:, lo:hi], ALU.mult)
 
         def fetch_raw(r, d, number):
             lo = HALF_V if r == 0 else 0
@@ -196,25 +196,27 @@ def tile_picked_grand_none_p_kernel(tc, x_words, x_scales, w1, gate, offs, cen, 
         for d in range(SHARED):
             nc.scalar.activation(raw0[d][:], y[0][:].indirect(lists[d][:, entries(OWN, V)]), COPY)
         fetch_scaled(term[2][:], 0, 2, V)
-        fetch_scaled(centre[0][:], 0, D, V)
+        fetch_scaled(centre0[:], 0, D, V)
         fetch_scaled(term[0][:], 0, 0, OWN)
-        nc.vector.tensor_tensor(partial[1][:], term[2][:], centre[0][:], ALU.add)
+        nc.vector.tensor_tensor(partial[1][:], term[2][:], centre0[:], ALU.add)
         fetch_scaled(term[1][:], 0, 1, OWN)
         nc.vector.tensor_tensor(partial[0][:], partial[1][:, 0:OWN], term[0][:], ALU.add)
-        fetch_scaled(centre[1][:], 1, D, V)
+        centre1 = keep.tile([P, V], F32, name="centre1")
+        fetch_scaled(centre1[:, HALF_V:V], 1, D, V, HALF_V)
         nc.vector.tensor_tensor(res[0][:, 0:OWN], partial[0][:], term[1][:], ALU.add)
         nc.sync.dma_start(out[0:P, 0:OWN], res[0][:, 0:OWN])
+        fetch_scaled(centre1[:, 0:HALF_V], 1, D, HALF_V)
         for d in range(D):
             fetch_raw(0, d, 2 + d)
         for d in range(D):
             weigh0(d)
             fetch_raw(1, d, (5, 6, 2)[d])
-        nc.vector.tensor_tensor(res[1][:, HALF_V:V], sum0[:, 0:HALF_V], centre[1][:, HALF_V:V], ALU.add)
+        nc.vector.tensor_tensor(res[1][:, HALF_V:V], sum0[:, 0:HALF_V], centre1[:, HALF_V:V], ALU.add)
         nc.sync.dma_start(out[P:N, HALF_V:V], res[1][:, HALF_V:V])
         nc.vector.tensor_tensor(res[0][:, OWN:V], sum0[:, block(2)], partial[1][:, OWN:V], ALU.add)
         nc.sync.dma_start(out[0:P, OWN:V], res[0][:, OWN:V])
         for d in range(D):
             weigh1(d)
         for b in range(2):
-            nc.vector.tensor_tensor(res[1][:, block(b)], sum1[b][:, 0:P], centre[1][:, block(b)], ALU.add)
+            nc.vector.tensor_tensor(res[1][:, block(b)], sum1[b][:, 0:P], centre1[:, block(b)], ALU.add)
             nc.sync.dma_start(out[P:N, block(b)], res[1][:, block(b)])

@@ -208,9 +208,12 @@ def tile_picked_grand_none_p_kernel(tc, x_words, x_scales, w1, gate, offs, cen, 
         fetch_scaled(centre1[:, 0:HALF_V], 1, D, HALF_V)
         for d in range(D):
             fetch_raw(0, d, 2 + d)
-        for d in range(D):
-            weigh0(d)
-            fetch_raw(1, d, (5, 6, 2)[d])
+        weigh0(0)
+        fetch_raw(1, 0, 5)
+        weigh0(1)
+        fetch_raw(1, 1, 6)
+        fetch_raw(1, 2, 2)
+        weigh0(2)
         nc.vector.tensor_tensor(res[1][:, HALF_V:V], sum0[:, 0:HALF_V], centre1[:, HALF_V:V], ALU.add)
         nc.sync.dma_start(out[P:N, HALF_V:V], res[1][:, HALF_V:V])
         nc.vector.tensor_tensor(res[0][:, OWN:V], sum0[:, block(2)], partial[1][:, OWN:V], ALU.add)

@@ -49,7 +49,7 @@ def tile_picked_grand_none_p_kernel(tc, x_words, x_scales, w1, gate, offs, cen, 
         offs_sb = keep.tile([P, S // PER_COLUMN], U16, name="offs_sb")
         lists = [keep.tile([P, V // PER_COLUMN], U16, name=f"list{d}") for d in range(D + 1)]
         words = keep.tile([P, T], U32, name="words", align_bytes=64)
-        scales = keep.tile([P, T], U8, name="scales", align_bytes=64)
+        scales = turns.tile([P, T], U8, name="scales", offset=0, align_bytes=64)
         plane = keep.tile([P, S], U8, name="plane", align_bytes=64)
         w_raw = [keep.tile([P, PACK, P], F32, name="w_raw0", align_bytes=64)]
         gate_rows = keep.tile([P, D, P], F32, name="gate_rows")
@@ -70,8 +70,6 @@ def tile_picked_grand_none_p_kernel(tc, x_words, x_scales, w1, gate, offs, cen, 
         nc.sync.dma_start(lists[0][:], pos1)
         nc.sync.dma_start(lists[1][:], pos2)
         nc.sync.dma_start(words[:].bitcast(I32), x_words[0].rearrange("p n t -> p (n t)").bitcast(I32))
-        w_raw.append(turns.tile([P, PACK, P], F32, name="w_raw1", offset=T - 2 * Q, align_bytes=64))
-        nc.sync.dma_start(w_raw[1][:], w_rows[:, :, P:N])
         nc.sync.dma_start(lists[2][:], pos3)
         nc.sync.dma_start(lists[D][:], cen)
 
@@ -97,6 +95,8 @@ def tile_picked_grand_none_p_kernel(tc, x_words, x_scales, w1, gate, offs, cen, 
         nc.vector.tensor_copy(picked_scales[:], scales[:].indirect(offs_sb[:]))
         for i in range(4):
             nc.sync.dma_start(plane[i:P:32, :].bitcast(I32), picked_scales[first_scale_row + i : P : 4, :].bitcast(I32))
+        w_raw.append(turns.tile([P, PACK, P], F32, name="w_raw1", offset=T - 4 * Q, align_bytes=64))
+        nc.sync.dma_start(w_raw[1][:], w_rows[:, :, P:N])
 
         quantize_w(0, w_bf0)
 
@@ -135,21 +135,30 @@ def tile_picked_grand_none_p_kernel(tc, x_words, x_scales, w1, gate, offs, cen, 
             )
             copy_out(y[m][:, lo:hi], acc[:, 0 : hi - lo])
 
-        for q in range(2):
+        for q in range(QUARTERS - 1):
             pick(q, keep.tile([P, Q], U32, name=f"picked{q}", align_bytes=64))
         quantize_w(1, w_bf1)
-        for q in range(2, 4):
-            pick(q, turns.tile([P, Q], U32, name=f"picked{q}", offset=T + 4 * Q * (q - 2), align_bytes=64))
+        pick(QUARTERS - 1, turns.tile([P, Q], U32, name="picked3", offset=T, align_bytes=64))
+        warm = bank(6, "warm")
+        for b in range(4):
+            nc.tensor.matmul_mx(
+                out=warm[:, block(b)],
+                lhsT=w_codes[0][:].bitcast(FP8X4),
+                lhsT_scale=w_scales[0][:],
+                rhs=w_codes[0][:].bitcast(FP8X4),
+                rhs_scale=plane[:, 0:P],
+                start=True,
+                stop=True,
+            )
         project(0, 0, 0, Q, nc.scalar.copy)
         project(0, 1, Q, 2 * Q, nc.scalar.copy)
-        project(1, 2, 0, Q, nc.scalar.copy)
-        project(1, 3, Q, 2 * Q, nc.scalar.copy)
-        project(0, 4, 2 * Q, 3 * Q, nc.vector.tensor_copy)
-        project(1, 5, 2 * Q, 3 * Q, nc.scalar.copy)
-        project(0, 6, 3 * Q, S - P, nc.vector.tensor_copy)
-        project(0, 7, S - P, S, nc.scalar.copy)
-        project(1, 0, 3 * Q, S - P, nc.vector.tensor_copy)
-        project(1, 1, S - P, S, nc.scalar.copy)
+        project(0, 2, 2 * Q, 3 * Q, nc.scalar.copy)
+        project(1, 3, 0, Q, nc.vector.tensor_copy)
+        project(1, 4, Q, 2 * Q, nc.scalar.copy)
+        project(0, 5, 3 * Q, S - P, nc.vector.tensor_copy)
+        project(0, 6, S - P, S, nc.scalar.copy)
+        project(1, 7, 2 * Q, 3 * Q, nc.scalar.copy)
+        project(1, 0, 3 * Q, S, nc.scalar.copy)
 
         raw0 = [keep.tile([P, P], F32, name=f"raw0_{d}") for d in range(SHARED)]
         raw1 = [keep.tile([P, HALF_V], F32, name=f"raw1_{d}") for d in range(D)]

@@ -15,6 +15,7 @@ HALF_V = V // 2
 LAST = BLOCKS - 1
 OWN = LAST * P
 SHARED = 2
+PLAIN = 128
 FLOPS = 2 * K * N * S
 
 F32 = mybir.dt.float32
@@ -157,8 +158,9 @@ def tile_picked_grand_none_p_kernel(tc, x_words, x_scales, w1, gate, offs, cen, 
         project(1, 4, Q, 2 * Q, nc.scalar.copy)
         project(0, 5, 3 * Q, S - P, nc.vector.tensor_copy)
         project(0, 6, S - P, S, nc.scalar.copy)
-        project(1, 7, 2 * Q, 3 * Q, nc.scalar.copy)
-        project(1, 0, 3 * Q, S, nc.scalar.copy)
+        project(1, 7, 2 * Q, 2 * Q + P, nc.vector.tensor_copy)
+        project(1, 0, 2 * Q + P, 3 * Q, nc.scalar.copy)
+        project(1, 1, 3 * Q, S, nc.scalar.copy)
 
         raw0 = [keep.tile([P, P], F32, name=f"raw0_{d}") for d in range(SHARED)]
         raw1 = [keep.tile([P, HALF_V], F32, name=f"raw1_{d}") for d in range(D)]
@@ -211,24 +213,23 @@ def tile_picked_grand_none_p_kernel(tc, x_words, x_scales, w1, gate, offs, cen, 
         fetch_scaled(term[1][:], 0, 1, OWN)
         nc.vector.tensor_tensor(partial[0][:], partial[1][:, 0:OWN], term[0][:], ALU.add)
         centre1 = keep.tile([P, V], F32, name="centre1")
-        fetch_scaled(centre1[:, HALF_V:V], 1, D, V, HALF_V)
+        fetch_scaled(centre1[:, PLAIN:V], 1, D, V, PLAIN)
         nc.vector.tensor_tensor(res[0][:, 0:OWN], partial[0][:], term[1][:], ALU.add)
         nc.sync.dma_start(out[0:P, 0:OWN], res[0][:, 0:OWN])
-        fetch_scaled(centre1[:, 0:HALF_V], 1, D, HALF_V)
         for d in range(D):
             fetch_raw(0, d, 2 + d)
-        weigh0(0)
-        fetch_raw(1, 0, 5)
-        weigh0(1)
-        fetch_raw(1, 1, 6)
-        fetch_raw(1, 2, 2)
-        weigh0(2)
+        for d in range(D):
+            weigh0(d)
+            fetch_raw(1, d, (5, 6, 2)[d])
         nc.vector.tensor_tensor(res[1][:, HALF_V:V], sum0[:, 0:HALF_V], centre1[:, HALF_V:V], ALU.add)
         nc.sync.dma_start(out[P:N, HALF_V:V], res[1][:, HALF_V:V])
+        weigh1(0)
+        weigh1(1)
+        nc.scalar.activation(raw1[1][:, 0:PLAIN], y[1][:].indirect(lists[D][:, entries(0, PLAIN)]), COPY)
+        nc.vector.tensor_tensor(centre1[:, 0:PLAIN], raw1[1][:, 0:PLAIN], factor[D][:, 0:PLAIN], ALU.mult)
         nc.vector.tensor_tensor(res[0][:, OWN:V], sum0[:, block(2)], partial[1][:, OWN:V], ALU.add)
         nc.sync.dma_start(out[0:P, OWN:V], res[0][:, OWN:V])
-        for d in range(D):
-            weigh1(d)
+        weigh1(2)
         for b in range(2):
             nc.vector.tensor_tensor(res[1][:, block(b)], sum1[b][:, 0:P], centre1[:, block(b)], ALU.add)
             nc.sync.dma_start(out[P:N, block(b)], res[1][:, block(b)])

@@ -14,8 +14,9 @@ Q = S // QUARTERS
 HALF_V = V // 2
 LAST = BLOCKS - 1
 OWN = LAST * P
-SHARED = 2
+SHARED = 1
 PLAIN = 128
+W_BYTES = PACK * P * 4
 FLOPS = 2 * K * N * S
 
 F32 = mybir.dt.float32
@@ -52,10 +53,10 @@ def tile_picked_grand_none_p_kernel(tc, x_words, x_scales, w1, gate, offs, cen, 
         words = keep.tile([P, T], U32, name="words", align_bytes=64)
         scales = turns.tile([P, T], U8, name="scales", offset=0, align_bytes=64)
         plane = keep.tile([P, S], U8, name="plane", align_bytes=64)
-        w_raw = [keep.tile([P, PACK, P], F32, name="w_raw0", align_bytes=64)]
+        w_raw = [turns.tile([P, PACK, P], F32, name="w_raw0", offset=T + W_BYTES, align_bytes=64)]
         gate_rows = keep.tile([P, D, P], F32, name="gate_rows")
         gate_t = keep.tile([P, D, BLOCKS], F32, name="gate_t")
-        centre_t = keep.tile([P, BLOCKS], F32, name="centre_t", tag="centre_then_w_bf1", align_bytes=64)
+        centre_t = keep.tile([P, BLOCKS], F32, name="centre_t", tag="centre_then_w_bf", align_bytes=64)
         ident = keep.tile([P, P], F32, name="ident")
 
         first_scale_row = P - SCALE_ROWS
@@ -67,11 +68,11 @@ def tile_picked_grand_none_p_kernel(tc, x_words, x_scales, w1, gate, offs, cen, 
         nc.scalar.dma_start(scales[first_scale_row:P, :].bitcast(I32), x_scales[0].bitcast(I32))
         nc.scalar.dma_start(gate_rows[first_gate_row:P, :, :], gate[:, 0, :].rearrange("d (b v) -> b d v", b=BLOCKS))
         w_rows = w1.rearrange("(p j) n -> p j n", j=PACK)
-        nc.sync.dma_start(w_raw[0][:], w_rows[:, :, 0:P])
         nc.sync.dma_start(lists[0][:], pos1)
         nc.sync.dma_start(lists[1][:], pos2)
-        nc.sync.dma_start(words[:].bitcast(I32), x_words[0].rearrange("p n t -> p (n t)").bitcast(I32))
         nc.sync.dma_start(lists[2][:], pos3)
+        nc.sync.dma_start(words[:].bitcast(I32), x_words[0].rearrange("p n t -> p (n t)").bitcast(I32))
+        nc.sync.dma_start(w_raw[0][:], w_rows[:, :, 0:P])
         nc.sync.dma_start(lists[D][:], cen)
 
         make_identity(nc, ident[:])
@@ -86,11 +87,10 @@ def tile_picked_grand_none_p_kernel(tc, x_words, x_scales, w1, gate, offs, cen, 
         w_codes = [keep.tile([P, P], U32, name=f"w_codes{m}", align_bytes=64) for m in range(2)]
         w_scales = [keep.tile([P, P], U8, name=f"w_scales{m}", align_bytes=64) for m in range(2)]
 
-        def quantize_w(m, w_bf):
-            nc.scalar.copy(w_bf[:].rearrange("p (c i) j -> p c j i", i=4), w_raw[m][:].rearrange("p j (c i) -> p c j i", i=4))
-            nc.vector.quantize_mx(out=w_codes[m][:].bitcast(FP8X4), scales=w_scales[m][:], in_=w_bf[:].rearrange("p n j -> p (n j)"))
+        def quantize_w(m, rounded):
+            nc.scalar.copy(rounded.rearrange("p (c i) j -> p c j i", i=4), w_raw[m][:].rearrange("p j (c i) -> p c j i", i=4))
+            nc.vector.quantize_mx(out=w_codes[m][:].bitcast(FP8X4), scales=w_scales[m][:], in_=rounded.rearrange("p n j -> p (n j)"))
 
-        w_bf0 = keep.tile([P, P, PACK], BF16, name="w_bf0", align_bytes=64)
 
         picked_scales = keep.tile([P, S], U8, name="picked_scales", align_bytes=64)
         nc.vector.tensor_copy(picked_scales[:], scales[:].indirect(offs_sb[:]))
@@ -98,8 +98,6 @@ def tile_picked_grand_none_p_kernel(tc, x_words, x_scales, w1, gate, offs, cen, 
             nc.sync.dma_start(plane[i:P:32, :].bitcast(I32), picked_scales[first_scale_row + i : P : 4, :].bitcast(I32))
         w_raw.append(turns.tile([P, PACK, P], F32, name="w_raw1", offset=T - 4 * Q, align_bytes=64))
         nc.sync.dma_start(w_raw[1][:], w_rows[:, :, P:N])
-
-        quantize_w(0, w_bf0)
 
         factor = [keep.tile([P, OWN if d < SHARED else V], F32, name=f"factor{d}") for d in range(D + 1)]
         for d in range(D + 1):
@@ -110,7 +108,7 @@ def tile_picked_grand_none_p_kernel(tc, x_words, x_scales, w1, gate, offs, cen, 
                 nc.tensor.transpose(spread[:, block(b)], columns[:, b : b + 1].to_broadcast([P, P]), ident[:])
             nc.scalar.copy(factor[d][:], spread[:, 0 : count * P])
 
-        w_bf1 = keep.tile([P, P, PACK], BF16, name="w_bf1", tag="centre_then_w_bf1", align_bytes=64)
+        w_bf = keep.tile([P, N, PACK], BF16, name="w_bf", tag="centre_then_w_bf", align_bytes=64)
 
         y = [
             turns.tile([P, S], F32, name="y0", offset=0, align_bytes=64),
@@ -136,37 +134,27 @@ def tile_picked_grand_none_p_kernel(tc, x_words, x_scales, w1, gate, offs, cen, 
             )
             copy_out(y[m][:, lo:hi], acc[:, 0 : hi - lo])
 
-        for q in range(QUARTERS - 1):
+        for q in range(2):
             pick(q, keep.tile([P, Q], U32, name=f"picked{q}", align_bytes=64))
-        quantize_w(1, w_bf1)
-        pick(QUARTERS - 1, turns.tile([P, Q], U32, name="picked3", offset=T, align_bytes=64))
-        warm = bank(6, "warm")
-        for b in range(4):
-            nc.tensor.matmul_mx(
-                out=warm[:, block(b)],
-                lhsT=w_codes[0][:].bitcast(FP8X4),
-                lhsT_scale=w_scales[0][:],
-                rhs=w_codes[0][:].bitcast(FP8X4),
-                rhs_scale=plane[:, 0:P],
-                start=True,
-                stop=True,
-            )
+        quantize_w(0, w_bf[:, block(0), :])
+        pick(2, turns.tile([P, Q], U32, name="picked2", offset=T + W_BYTES, align_bytes=64))
+        pick(3, turns.tile([P, Q], U32, name="picked3", offset=T + W_BYTES + 4 * Q, align_bytes=64))
+        quantize_w(1, w_bf[:, block(1), :])
         project(0, 0, 0, Q, nc.scalar.copy)
         project(0, 1, Q, 2 * Q, nc.scalar.copy)
         project(0, 2, 2 * Q, 3 * Q, nc.scalar.copy)
-        project(1, 3, 0, Q, nc.vector.tensor_copy)
-        project(1, 4, Q, 2 * Q, nc.scalar.copy)
         project(0, 5, 3 * Q, S - P, nc.vector.tensor_copy)
         project(0, 6, S - P, S, nc.scalar.copy)
-        project(1, 7, 2 * Q, 2 * Q + P, nc.vector.tensor_copy)
-        project(1, 0, 2 * Q + P, 3 * Q, nc.scalar.copy)
+        project(1, 3, 0, Q, nc.scalar.copy)
+        project(1, 4, Q, 2 * Q, nc.scalar.copy)
+        project(1, 7, 2 * Q, 3 * Q, nc.scalar.copy)
         project(1, 1, 3 * Q, S, nc.scalar.copy)
 
         raw0 = [keep.tile([P, P], F32, name=f"raw0_{d}") for d in range(SHARED)]
         raw1 = [keep.tile([P, HALF_V], F32, name=f"raw1_{d}") for d in range(D)]
         weighted = [[keep.tile([P, 3 * P], F32, name=f"weighted{r}_{d}") for d in range(D)] for r in range(2)]
         term = [keep.tile([P, OWN if d < SHARED else V], F32, name=f"term{d}") for d in range(D)]
-        partial = [keep.tile([P, OWN], F32, name="partial0"), keep.tile([P, V], F32, name="partial1")]
+        partial = [keep.tile([P, V], F32, name="partial0"), keep.tile([P, V], F32, name="partial1")]
         centre0 = keep.tile([P, V], F32, name="centre0")
         res = [keep.tile([P, V], F32, name=f"res{m}") for m in range(2)]
         turned = {}
@@ -208,13 +196,13 @@ def tile_picked_grand_none_p_kernel(tc, x_words, x_scales, w1, gate, offs, cen, 
             nc.scalar.activation(raw0[d][:], y[0][:].indirect(lists[d][:, entries(OWN, V)]), COPY)
         fetch_scaled(term[2][:], 0, 2, V)
         fetch_scaled(centre0[:], 0, D, V)
-        fetch_scaled(term[0][:], 0, 0, OWN)
+        fetch_scaled(term[1][:], 0, 1, V)
         nc.vector.tensor_tensor(partial[1][:], term[2][:], centre0[:], ALU.add)
-        fetch_scaled(term[1][:], 0, 1, OWN)
-        nc.vector.tensor_tensor(partial[0][:], partial[1][:, 0:OWN], term[0][:], ALU.add)
+        fetch_scaled(term[0][:], 0, 0, OWN)
+        nc.vector.tensor_tensor(partial[0][:], partial[1][:], term[1][:], ALU.add)
         centre1 = keep.tile([P, V], F32, name="centre1")
         fetch_scaled(centre1[:, PLAIN:V], 1, D, V, PLAIN)
-        nc.vector.tensor_tensor(res[0][:, 0:OWN], partial[0][:], term[1][:], ALU.add)
+        nc.vector.tensor_tensor(res[0][:, 0:OWN], partial[0][:, 0:OWN], term[0][:], ALU.add)
         nc.sync.dma_start(out[0:P, 0:OWN], res[0][:, 0:OWN])
         for d in range(D):
             fetch_raw(0, d, 2 + d)
@@ -227,7 +215,7 @@ def tile_picked_grand_none_p_kernel(tc, x_words, x_scales, w1, gate, offs, cen, 
         weigh1(1)
         nc.scalar.activation(raw1[1][:, 0:PLAIN], y[1][:].indirect(lists[D][:, entries(0, PLAIN)]), COPY)
         nc.vector.tensor_tensor(centre1[:, 0:PLAIN], raw1[1][:, 0:PLAIN], factor[D][:, 0:PLAIN], ALU.mult)
-        nc.vector.tensor_tensor(res[0][:, OWN:V], sum0[:, block(2)], partial[1][:, OWN:V], ALU.add)
+        nc.vector.tensor_tensor(res[0][:, OWN:V], sum0[:, block(2)], partial[0][:, OWN:V], ALU.add)
         nc.sync.dma_start(out[0:P, OWN:V], res[0][:, OWN:V])
         weigh1(2)
         for b in range(2):

@@ -16,7 +16,6 @@ LAST = BLOCKS - 1
 OWN = LAST * P
 SHARED = 1
 PLAIN = 128
-W_BYTES = PACK * P * 4
 FLOPS = 2 * K * N * S
 
 F32 = mybir.dt.float32
@@ -53,7 +52,10 @@ def tile_picked_grand_none_p_kernel(tc, x_words, x_scales, w1, gate, offs, cen, 
         words = keep.tile([P, T], U32, name="words", align_bytes=64)
         scales = turns.tile([P, T], U8, name="scales", offset=0, align_bytes=64)
         plane = keep.tile([P, S], U8, name="plane", align_bytes=64)
-        w_raw = [turns.tile([P, PACK, P], F32, name="w_raw0", offset=T + W_BYTES, align_bytes=64)]
+        w_raw = [
+            turns.tile([P, PACK, P], F32, name="w_raw0", offset=T, align_bytes=64),
+            keep.tile([P, PACK, P], F32, name="w_raw1", align_bytes=64),
+        ]
         gate_rows = keep.tile([P, D, P], F32, name="gate_rows")
         gate_t = keep.tile([P, D, BLOCKS], F32, name="gate_t")
         centre_t = keep.tile([P, BLOCKS], F32, name="centre_t", tag="centre_then_w_bf", align_bytes=64)
@@ -69,10 +71,11 @@ def tile_picked_grand_none_p_kernel(tc, x_words, x_scales, w1, gate, offs, cen, 
         nc.scalar.dma_start(gate_rows[first_gate_row:P, :, :], gate[:, 0, :].rearrange("d (b v) -> b d v", b=BLOCKS))
         w_rows = w1.rearrange("(p j) n -> p j n", j=PACK)
         nc.sync.dma_start(lists[0][:], pos1)
-        nc.sync.dma_start(lists[1][:], pos2)
-        nc.sync.dma_start(lists[2][:], pos3)
         nc.sync.dma_start(words[:].bitcast(I32), x_words[0].rearrange("p n t -> p (n t)").bitcast(I32))
+        nc.sync.dma_start(lists[1][:], pos2)
         nc.sync.dma_start(w_raw[0][:], w_rows[:, :, 0:P])
+        nc.sync.dma_start(w_raw[1][:], w_rows[:, :, P:N])
+        nc.sync.dma_start(lists[2][:], pos3)
         nc.sync.dma_start(lists[D][:], cen)
 
         make_identity(nc, ident[:])
@@ -96,8 +99,6 @@ def tile_picked_grand_none_p_kernel(tc, x_words, x_scales, w1, gate, offs, cen, 
         nc.vector.tensor_copy(picked_scales[:], scales[:].indirect(offs_sb[:]))
         for i in range(4):
             nc.sync.dma_start(plane[i:P:32, :].bitcast(I32), picked_scales[first_scale_row + i : P : 4, :].bitcast(I32))
-        w_raw.append(turns.tile([P, PACK, P], F32, name="w_raw1", offset=T - 4 * Q, align_bytes=64))
-        nc.sync.dma_start(w_raw[1][:], w_rows[:, :, P:N])
 
         factor = [keep.tile([P, OWN if d < SHARED else V], F32, name=f"factor{d}") for d in range(D + 1)]
         for d in range(D + 1):
@@ -137,8 +138,8 @@ def tile_picked_grand_none_p_kernel(tc, x_words, x_scales, w1, gate, offs, cen, 
         for q in range(2):
             pick(q, keep.tile([P, Q], U32, name=f"picked{q}", align_bytes=64))
         quantize_w(0, w_bf[:, block(0), :])
-        pick(2, turns.tile([P, Q], U32, name="picked2", offset=T + W_BYTES, align_bytes=64))
-        pick(3, turns.tile([P, Q], U32, name="picked3", offset=T + W_BYTES + 4 * Q, align_bytes=64))
+        pick(2, turns.tile([P, Q], U32, name="picked2", offset=T, align_bytes=64))
+        pick(3, turns.tile([P, Q], U32, name="picked3", offset=T + 4 * Q, align_bytes=64))
         quantize_w(1, w_bf[:, block(1), :])
         project(0, 0, 0, Q, nc.scalar.copy)
         project(0, 1, Q, 2 * Q, nc.scalar.copy)

from contextlib import ExitStack

import concourse.mybir as mybir
from concourse.masks import make_identity

K, T, S, D, V, N = 512, 4096, 1024, 3, 512, 256
P = 128
PACK = 4
BLOCKS = V // P
SCALE_ROWS = K // 32
PER_COLUMN = 16
QUARTERS = 4
Q = S // QUARTERS
HALF_V = V // 2
LAST = BLOCKS - 1
OWN = LAST * P
SHARED = 1
PLAIN = 128
FLOPS = 2 * K * N * S

F32 = mybir.dt.float32
BF16 = mybir.dt.bfloat16
I32 = mybir.dt.int32
U32 = mybir.dt.uint32
U16 = mybir.dt.uint16
U8 = mybir.dt.uint8
FP8X4 = mybir.dt.float8_e4m3fn_x4
ALU = mybir.AluOpType
COPY = mybir.ActivationFunctionType.Copy


def block(b):
    return slice(b * P, (b + 1) * P)


def entries(lo, hi):
    return slice(lo // PER_COLUMN, hi // PER_COLUMN)


def tile_picked_grand_none_p_kernel(tc, x_words, x_scales, w1, gate, offs, cen, pos1, pos2, pos3, out):
    nc = tc.nc
    with ExitStack() as ctx:
        keep = ctx.enter_context(tc.tile_pool(name="keep", bufs=1))
        turns = ctx.enter_context(tc.tile_pool(name="turns", bufs=1))
        psum = ctx.enter_context(tc.psum_pool(name="psum", bufs=1))

        def bank(number, name):
            return psum.tile([P, 512], F32, name=name, tag=f"bank{number}")

        offs_sb = keep.tile([P, S // PER_COLUMN], U16, name="offs_sb")
        lists = [keep.tile([P, V // PER_COLUMN], U16, name=f"list{d}") for d in range(D + 1)]
        words = keep.tile([P, T], U32, name="words", align_bytes=64)
        scales = turns.tile([P, T], U8, name="scales", offset=0, align_bytes=64)
        plane = keep.tile([P, S], U8, name="plane", align_bytes=64)
        w_raw = [
            turns.tile([P, PACK, P], F32, name="w_raw0", offset=T, align_bytes=64),
            keep.tile([P, PACK, P], F32, name="w_raw1", align_bytes=64),
        ]
        gate_rows = keep.tile([P, D, P], F32, name="gate_rows")
        gate_t = keep.tile([P, D, BLOCKS], F32, name="gate_t")
        centre_t = keep.tile([P, BLOCKS], F32, name="centre_t", tag="centre_then_w_bf", align_bytes=64)
        ident = keep.tile([P, P], F32, name="ident")

        first_scale_row = P - SCALE_ROWS
        first_gate_row = P - BLOCKS
        nc.vector.memset(scales[0:first_scale_row, :].bitcast(I32), 0)
        nc.vector.memset(gate_rows[0:first_gate_row, :, :], 0.0)
        nc.vector.memset(plane[:].bitcast(I32), 0)
        nc.sync.dma_start(offs_sb[:], offs)
        nc.scalar.dma_start(scales[first_scale_row:P, :].bitcast(I32), x_scales[0].bitcast(I32))
        nc.scalar.dma_start(gate_rows[first_gate_row:P, :, :], gate[:, 0, :].rearrange("d (b v) -> b d v", b=BLOCKS))
        w_rows = w1.rearrange("(p j) n -> p j n", j=PACK)
        nc.sync.dma_start(lists[0][:], pos1)
        nc.sync.dma_start(words[:].bitcast(I32), x_words[0].rearrange("p n t -> p (n t)").bitcast(I32))
        nc.sync.dma_start(lists[1][:], pos2)
        nc.sync.dma_start(w_raw[0][:], w_rows[:, :, 0:P])
        nc.sync.dma_start(w_raw[1][:], w_rows[:, :, P:N])
        nc.sync.dma_start(lists[2][:], pos3)
        nc.sync.dma_start(lists[D][:], cen)

        make_identity(nc, ident[:])
        gate_turned = bank(7, "gate_turned")
        for d in range(D):
            nc.tensor.transpose(gate_turned[:, block(d)], gate_rows[:, d, :], ident[:])
        for d in range(D):
            nc.tensor.matmul(gate_turned[:, block(D)], gate_rows[:, d, :], ident[:], start=d == 0, stop=d == D - 1, is_transpose=True)
        nc.scalar.activation(gate_t[:], gate_turned[:].rearrange("p (d r) -> p d r", r=P)[:, 0:D, first_gate_row:P], COPY)
        nc.scalar.activation(centre_t[:], gate_turned[:, D * P + first_gate_row : (D + 1) * P], COPY, scale=-1.0, bias=1.0)

        w_codes = [keep.tile([P, P], U32, name=f"w_codes{m}", align_bytes=64) for m in range(2)]
        w_scales = [keep.tile([P, P], U8, name=f"w_scales{m}", align_bytes=64) for m in range(2)]

        def quantize_w(m, rounded):
            nc.scalar.copy(rounded.rearrange("p (c i) j -> p c j i", i=4), w_raw[m][:].rearrange("p j (c i) -> p c j i", i=4))
            nc.vector.quantize_mx(out=w_codes[m][:].bitcast(FP8X4), scales=w_scales[m][:], in_=rounded.rearrange("p n j -> p (n j)"))


        picked_scales = keep.tile([P, S], U8, name="picked_scales", align_bytes=64)
        nc.vector.tensor_copy(picked_scales[:], scales[:].indirect(offs_sb[:]))
        for i in range(4):
            nc.sync.dma_start(plane[i:P:32, :].bitcast(I32), picked_scales[first_scale_row + i : P : 4, :].bitcast(I32))

        factor = [keep.tile([P, OWN if d < SHARED else V], F32, name=f"factor{d}") for d in range(D + 1)]
        for d in range(D + 1):
            spread = bank(d, f"spread{d}")
            columns = gate_t[:, d, :] if d < D else centre_t[:]
            count = LAST if d < SHARED else BLOCKS
            for b in range(count):
                nc.tensor.transpose(spread[:, block(b)], columns[:, b : b + 1].to_broadcast([P, P]), ident[:])
            nc.scalar.copy(factor[d][:], spread[:, 0 : count * P])

        w_bf = keep.tile([P, N, PACK], BF16, name="w_bf", tag="centre_then_w_bf", align_bytes=64)

        y = [
            turns.tile([P, S], F32, name="y0", offset=0, align_bytes=64),
            keep.tile([P, S], F32, name="y1"),
        ]
        picked = []

        def pick(q, tile):
            picked.append(tile)
            nc.vector.tensor_copy(picked[q][:], words[:].indirect(offs_sb[:, entries(q * Q, (q + 1) * Q)]))

        def project(m, number, lo, hi, copy_out):
            q = lo // Q
            acc = bank(number, f"acc{m}_{lo}")
            nc.tensor.matmul_mx(
                out=acc[:, 0 : hi - lo],
                lhsT=w_codes[m][:].bitcast(FP8X4),
                lhsT_scale=w_scales[m][:],
                rhs=picked[q][:, lo - q * Q : hi - q * Q].bitcast(FP8X4),
                rhs_scale=plane[:, lo:hi],
                start=True,
                stop=True,
            )
            copy_out(y[m][:, lo:hi], acc[:, 0 : hi - lo])

        for q in range(2):
            pick(q, keep.tile([P, Q], U32, name=f"picked{q}", align_bytes=64))
        quantize_w(0, w_bf[:, block(0), :])
        pick(2, turns.tile([P, Q], U32, name="picked2", offset=T, align_bytes=64))
        pick(3, turns.tile([P, Q], U32, name="picked3", offset=T + 4 * Q, align_bytes=64))
        quantize_w(1, w_bf[:, block(1), :])
        project(0, 0, 0, Q, nc.scalar.copy)
        project(0, 1, Q, 2 * Q, nc.scalar.copy)
        project(0, 2, 2 * Q, 3 * Q, nc.scalar.copy)
        project(0, 5, 3 * Q, S - P, nc.vector.tensor_copy)
        project(0, 6, S - P, S, nc.scalar.copy)
        project(1, 3, 0, Q, nc.scalar.copy)
        project(1, 4, Q, 2 * Q, nc.scalar.copy)
        project(1, 7, 2 * Q, 3 * Q, nc.scalar.copy)
        project(1, 1, 3 * Q, S, nc.scalar.copy)

        raw0 = [keep.tile([P, P], F32, name=f"raw0_{d}") for d in range(SHARED)]
        raw1 = [keep.tile([P, HALF_V], F32, name=f"raw1_{d}") for d in range(D)]
        weighted = [[keep.tile([P, 3 * P], F32, name=f"weighted{r}_{d}") for d in range(D)] for r in range(2)]
        term = [keep.tile([P, OWN if d < SHARED else V], F32, name=f"term{d}") for d in range(D)]
        partial = [keep.tile([P, V], F32, name="partial0"), keep.tile([P, V], F32, name="partial1")]
        centre0 = keep.tile([P, V], F32, name="centre0")
        res = [keep.tile([P, V], F32, name=f"res{m}") for m in range(2)]
        turned = {}

        def fetch_scaled(dst, m, d, hi, lo=0):
            nc.vector.tensor_tensor(dst, y[m][:].indirect(lists[d][:, entries(lo, hi)]), factor[d][:, lo:hi], ALU.mult)

        def fetch_raw(r, d, number):
            lo = HALF_V if r == 0 else 0
            nc.scalar.activation(raw1[d][:], y[1][:].indirect(lists[d][:, entries(lo, lo + HALF_V)]), COPY)
            turned[r, d] = bank(number, f"turned{r}_{d}")
            if r == 0 and d < SHARED:
                nc.tensor.transpose(turned[r, d][:, block(2)], raw0[d][:], ident[:])
            for b in range(2):
                nc.tensor.transpose(turned[r, d][:, block(b)], raw1[d][:, block(b)], ident[:])

        def weigh(r, d, lo, hi, b):
            nc.scalar.activation(weighted[r][d][:, lo:hi], turned[r, d][:, lo:hi], COPY, scale=gate_t[:, d, b : b + 1])

        def turn_back(dst, src, start, stop):
            nc.tensor.matmul(dst, src, ident[:], start=start, stop=stop, is_transpose=True)

        sum0 = bank(7, "sum0")
        sum1 = [bank(b, f"sum1_{b}") for b in range(2)]

        def weigh0(d):
            count = 3 if d < SHARED else 2
            weigh(0, d, 0, P, 2)
            weigh(0, d, P, count * P, LAST)
            for i in range(count):
                turn_back(sum0[:, block(i)], weighted[0][d][:, block(i)], d == 0 and i == 0, d == D - 1 and i == count - 1)

        def weigh1(d):
            for b in range(2):
                weigh(1, d, b * P, (b + 1) * P, b)
                turn_back(sum1[b][:, 0:P], weighted[1][d][:, block(b)], d == 0, d == D - 1)

        for d in range(SHARED):
            nc.scalar.activation(raw0[d][:], y[0][:].indirect(lists[d][:, entries(OWN, V)]), COPY)
        fetch_scaled(term[2][:], 0, 2, V)
        fetch_scaled(centre0[:], 0, D, V)
        fetch_scaled(term[1][:], 0, 1, V)
        nc.vector.tensor_tensor(partial[1][:], term[2][:], centre0[:], ALU.add)
        fetch_scaled(term[0][:], 0, 0, OWN)
        nc.vector.tensor_tensor(partial[0][:], partial[1][:], term[1][:], ALU.add)
        centre1 = keep.tile([P, V], F32, name="centre1")
        fetch_scaled(centre1[:, PLAIN:V], 1, D, V, PLAIN)
        nc.vector.tensor_tensor(res[0][:, 0:OWN], partial[0][:, 0:OWN], term[0][:], ALU.add)
        nc.sync.dma_start(out[0:P, 0:OWN], res[0][:, 0:OWN])
        for d in range(D):
            fetch_raw(0, d, 2 + d)
        for d in range(D):
            weigh0(d)
            fetch_raw(1, d, (5, 6, 2)[d])
        nc.vector.tensor_tensor(res[1][:, HALF_V:V], sum0[:, 0:HALF_V], centre1[:, HALF_V:V], ALU.add)
        nc.sync.dma_start(out[P:N, HALF_V:V], res[1][:, HALF_V:V])
        weigh1(0)
        weigh1(1)
        nc.scalar.activation(raw1[1][:, 0:PLAIN], y[1][:].indirect(lists[D][:, entries(0, PLAIN)]), COPY)
        nc.vector.tensor_tensor(centre1[:, 0:PLAIN], raw1[1][:, 0:PLAIN], factor[D][:, 0:PLAIN], ALU.mult)
        nc.vector.tensor_tensor(res[0][:, OWN:V], sum0[:, block(2)], partial[0][:, OWN:V], ALU.add)
        nc.sync.dma_start(out[0:P, OWN:V], res[0][:, OWN:V])
        weigh1(2)
        for b in range(2):
            nc.vector.tensor_tensor(res[1][:, block(b)], sum1[b][:, 0:P], centre1[:, block(b)], ALU.add)
            nc.sync.dma_start(out[P:N, block(b)], res[1][:, block(b)])
